import numpy as np, ml_dtypes
CORES = [16,17,18,19,32,33,34,35]
N = 8
BF = ml_dtypes.bfloat16
W, A, S, CAP, RO = 4096, 256, 1, 64, 3
P, BL = A // S, W // CAP
WT = 2 * np.arange(16) + 1
def counts(rng, fat):
    return np.where(fat, rng.integers(9, 17, fat.shape), rng.integers(0, 9, fat.shape))
def cols(rng, n, top):
    on = np.argsort(rng.random((N, 8, 16, W)), axis=2) < n[:, :, None, :]
    return np.where(on, 1 + (top * rng.random((N, 8, 16, W))).astype(np.int64), 0)
def lines(rng, fat, share):
    o = np.argsort(np.where(fat, 0.0, 1.0) + 0.5 * rng.random((N, 8, W)), axis=-1); nf = np.add.reduce(fat.astype(np.int64), axis=-1)[:, :, None, None]
    v = rng.random((N, 8, 16, A))
    k = np.where(rng.random((N, 8, 16, A)) < share, (v * nf).astype(np.int64), nf + (v * (W - nf)).astype(np.int64))
    return np.take_along_axis(o, k.reshape(N, 8, 16 * A), 2).reshape(N, 8, 16, A)
def hop(e, u):
    return (((e * u) >> 5) + e) & (W - 1)
def first(X):
    u = np.add.reduce(X * WT.reshape(1, 1, 16, 1), axis=2) & (W - 1); h = hop(np.arange(W).reshape(1, 1, W), u)
    y = np.take_along_axis(X, h[:, :, None, :], 3)
    return np.add.reduce(np.sign(y - X), axis=2), np.add.reduce((X > 0).astype(np.int64), axis=2)
def top16(s):
    v = np.full(16, 255); d = (65280 - s) & (W - 1)
    for w in range(15, -1, -1):
        c = min(254, d // (2 * w + 1)); v[w] -= c; d -= c * (2 * w + 1)
    return v
def pack(X, E, M):
    return {"xt": X.reshape(N, 128, W).astype(np.float32).astype(BF), "led": E.reshape(N, 128, A).astype(np.int32), "mk": M.reshape(N, 128, A).astype(np.float32).astype(BF)}
def setup_inputs(rng):
    fat = rng.random((N, 8, W)) < rng.choice(np.array([0.3, 0.5, 0.7]), (N, 8, 1))
    X = cols(rng, counts(rng, fat), 255)
    share = rng.choice(np.array([0.01, 0.05, 0.15, 0.6]), (N, 8, 1, A)) * rng.choice(np.array([0.2, 1.0, 1.5]), (N, 8, 1, 1))
    return pack(X, lines(rng, fat, share), rng.integers(0, 2, (N, 8, 16, A)))
def setup_inputs_spread(rng):
    fat = rng.random((N, 8, W)) < rng.choice(np.array([0.2, 0.5, 0.8]), (N, 8, 1))
    top = np.minimum(np.exp2(8 * rng.random((N, 8, 1, W))).astype(np.int64), 255)
    X = cols(rng, counts(rng, fat), top)
    E = lines(rng, fat, rng.choice(np.array([0.01, 0.05, 0.2, 0.7]), (N, 8, 1, A)))
    low = (W * rng.random((N, 8, 16, A)) ** 4).astype(np.int64); E = np.where(rng.random((N, 8, 1, A)) < 0.25, low, E)
    return pack(X, E, (rng.random((N, 8, 16, A)) < rng.random((N, 8, 1, A))).astype(np.int64))
def setup_inputs_ends(rng):
    kind = rng.integers(0, 3, (N, 8, 1, W))
    X = np.where(kind == 0, 0, np.where(kind == 1, 255, 255 * rng.integers(0, 2, (N, 8, 16, W))))
    X[..., 1] = 1; X[..., hop(1, 256)] = 255
    X[..., 2] = 255; X[..., hop(2, 65280 & (W - 1))] = 0
    X[..., W - 2] = 254; X[..., hop(W - 2, 65024 & (W - 1))] = 255
    X[..., W - 1] = top16(W - 1); X[..., hop(W - 1, W - 1)] = 0
    sh = (N, 8, 16, A)
    other = np.where(rng.random(sh) < 0.5, rng.choice(np.array([1, 2, W - 2]), sh), rng.integers(0, W, sh))
    E = np.where(rng.random(sh) < 0.7, (W - 1) * rng.integers(0, 2, sh), other)
    M = (rng.random(sh) < rng.choice(np.array([0.0, 0.5, 1.0]), (N, 8, 1, A))).astype(np.int64)
    i = np.arange(P) * S; q = N - 1
    for r in (0, q):
        for g in range(8):
            k = 2 * rng.integers(0, 8, P); E[r, g, k, i] = W - 1; M[r, g, k, i] = 1
    E[1, 0, :, 0::S] = 0; M[1, 0, :, 0::S] = 0
    E[q, 0, :, 0] = 0; M[q, 0, :, 0] = 0
    a, b, c, d = int(i[CAP - 1]), int(i[P - 1]), int(i[P - 2]), int(i[3])
    E[q, 7, :, a] = W - 1; M[q, 7, :, a] = 1
    E[q, 7, :, b] = 0; M[q, 7, :, b] = 0; E[q, 7, 14:, b] = W - 1; M[q, 7, 14:, b] = 1
    E[q, 7, :, c] = 0; M[q, 7, :, c] = 0; E[q, 7, 14, c] = W - 2; M[q, 7, 14, c] = 1; E[q, 7, 15, c] = 1
    E[:, 7, 0::2, d] = 2; M[:, 7, 0::2, d] = 1; E[:, 7, 1::2, d] = W - 1; M[:, 7, 1::2, d] = 0
    return pack(X, E, M)
def setup_inputs_corners(rng):
    fat = rng.random((N, 8, W)) < 0.5; X = cols(rng, counts(rng, fat), 255)
    E = lines(rng, fat, 0.1); M = rng.integers(0, 2, (N, 8, 16, A)); g, n = first(X)
    room = (0, 1, CAP - 1, CAP, CAP + 1, P, CAP, P - 1); even = np.arange(16)[:, None] % 2 == 0
    for q in range(N):
        for b in range(8):
            gg = g[q, b]; hot = np.flatnonzero((n[q, b] >= 9) & (gg != 0)); thin = np.flatnonzero(n[q, b] <= 8)
            c = int(rng.choice(np.array(room)))
            if q == 0: c = room[b]
            if q == N - 1: c = room[(b + 4) % 8]
            o = np.concatenate([np.array([P - 1]), rng.permutation(P - 1)]); yes = o[:c]; z = np.zeros((1, P), bool); z[0, o[c:]] = True
            e = np.where(rng.random((16, P)) < 0.2, (W - 1) * rng.integers(0, 2, (16, P)), rng.integers(0, W, (16, P)))
            m = (rng.random((16, P)) < rng.choice(np.array([0.0, 0.5, 1.0]), (1, P))).astype(np.int64)
            ge = gg[e]; m = np.where(even & z & (ge != 0), (ge > 0).astype(np.int64), m)
            e = np.where(~even & z, rng.choice(thin, (16, P)), e)
            k = 2 * rng.integers(0, 8, c); hh = rng.choice(hot, c); e[k, yes] = hh; m[k, yes] = (gg[hh] < 0).astype(np.int64)
            E[q, b, :, 0::S] = e; M[q, b, :, 0::S] = m
    return pack(X, E, M)
def setup_inputs_ties(rng):
    fat = rng.random((N, 8, W)) < 0.5
    n = np.where(fat, np.where(rng.random((N, 8, W)) < 0.8, 9, 16), 8); X = cols(rng, n, rng.choice(np.array([1, 2, 3]), (N, 8, 1, W)))
    E = lines(rng, fat, rng.choice(np.array([0.02, 0.2, 0.5]), (N, 8, 1, A)))
    E = np.take_along_axis(E, rng.integers(0, 3, (N, 8, 16, A)), 2)
    return pack(X, E, (rng.random((N, 8, 16, A)) < rng.choice(np.array([0.1, 0.5, 0.9]), (N, 8, 1, A))).astype(np.int64))
def setup_inputs_deep(rng):
    fat = rng.random((N, 8, W)) < 0.5; X = cols(rng, counts(rng, fat), 255)
    X[..., 0] = 0
    X[..., 3] = 253; X[..., hop(3, 64768 & (W - 1))] = 255
    X[..., 5] = 252; X[..., hop(5, 64512 & (W - 1))] = 255
    X[..., 7] = 255; X[..., hop(7, 65280 & (W - 1))] = 255; X[..., hop(7, 62976 & (W - 1))] = 255
    X[..., 11] = W >> 8
    X[..., W - 3] = top16(W - 21); X[..., hop(W - 3, W - 21)] = 0; X[..., hop(W - 3, W - 21) + 1] = 255
    X[..., 1001] = 255; X[..., 0, 1001] = 254; X[..., hop(1001, 65279 & (W - 1))] = 0
    X[..., 13] = 0; X[..., 7:, 13] = 255; X[..., hop(13, 52785 & (W - 1))] = 0
    X[..., 17] = 0; X[..., :9, 17] = 255; X[..., hop(17, 20655 & (W - 1))] = 0
    E = lines(rng, fat, 0.1); M = rng.integers(0, 2, (N, 8, 16, A)); s, n = first(X)
    h = hop(np.arange(W).reshape(1, 1, W), np.add.reduce(X * WT.reshape(1, 1, 16, 1), axis=2) & (W - 1))
    kind = np.argsort(rng.random((N, 8, P)), axis=-1) % 7
    for q in range(N):
        for b in range(8):
            if b in (1, 6):
                far = np.arange(W) >= (W >> 2); nn = n[q, b]; hh = h[q, b]
                thin = np.flatnonzero((nn <= 8) & far); hot = np.flatnonzero((nn >= 9) & (s[q, b] < 0) & (nn[hh] <= 8) & far[hh])
                E[q, b] = rng.choice(thin, (16, A))
                c = int(rng.integers(CAP >> 3, (CAP >> 2) + 1)); i = S * rng.permutation(P)[:c]; k = 2 * rng.integers(0, 8, c)
                E[q, b, k, i] = rng.choice(hot, c); M[q, b, k, i] = 1
                continue
            for v in range(1, 7):
                i = S * np.flatnonzero(kind[q, b] == v); k = 2 * rng.integers(0, 8, len(i))
                E[q, b, :, i] = 0; M[q, b, :, i] = 0
                if v == 1:
                    for w, e, m in ((0, 3, 1), (2, 3, 1), (4, 3, 1), (6, 5, 1), (7, 7, 1), (8, 7, 0), (9, 7, 1), (10, 7, 0), (11, 7, 1), (12, 7, 0), (13, 7, 0), (14, 7, 0)):
                        E[q, b, w, i] = e; M[q, b, w, i] = m
                elif v == 2:
                    E[q, b, k, i] = W - 3; M[q, b, k, i] = 1
                elif v == 3:
                    E[q, b, k, i] = 11; M[q, b, k, i] = 1; E[q, b, k + 1, i] = 7
                else:
                    E[q, b, k, i] = (1001, 13, 17)[v - 4]; M[q, b, k, i] = 1
    return pack(X, E, M)
def check_inputs(d):
    bad = []
    for k, lo, hi in (("xt", 0, 255), ("led", 0, W - 1), ("mk", 0, 1)):
        v = np.asarray(d[k]).astype(np.float64)
        if np.min(v) < lo or np.max(v) > hi or np.any(v != np.floor(v)): bad.append("range of " + k)
    return bad
def look(X, ix):
    return np.take_along_axis(X, ix.reshape(N, 8, 1, 16 * P), 3).reshape(N, 8, 16, 16, P)
def reference(xt, led, mk):
    X = xt.astype(np.float32).astype(np.int64).reshape(N, 8, 16, W)
    E = led.astype(np.int64).reshape(N, 8, 16, A); M = mk.astype(np.float32).astype(np.int64).reshape(N, 8, 16, A)
    kappa = np.zeros((N, 1, 1, 1), np.int64); ks = np.arange(16).reshape(1, 1, 16, 1)
    for t in range(RO):
        c = t % S; e = E[:, :, :, c::S].copy(); m = M[:, :, :, c::S].copy()
        x = look(X, e); q = x.copy(); b = np.zeros((N, 8, 16, P), np.int64)
        for k in range(16):
            mm = m[:, :, k][:, :, None, :]
            if k % 2 == 0: b = b + mm * x[:, :, :, k]
            else:
                q[:, :, :, k] = np.minimum(b, x[:, :, :, k]); b = b - mm * q[:, :, :, k]
        u = np.add.reduce(WT.reshape(1, 1, 16, 1, 1) * q, axis=2) & (W - 1)
        h = (((e * u) >> 5) + e + kappa) & (W - 1)
        g = np.add.reduce(np.sign(look(X, h) - q), axis=2); over = np.add.reduce((q > 0).astype(np.int64), axis=2)
        con = (over >= 9) & (((m == 1) & (g < 0)) | ((m == 0) & (g > 0)))
        best = np.argmax(np.where(con, np.abs(g), 0), axis=2)
        flip = np.any(con, axis=2)
        win = flip[:, :, None, :] & (ks == best[:, :, None, :])
        E[:, :, :, c::S] = np.where(win, h, e); M[:, :, :, c::S] = np.where(win, 1 - m, m)
        f = flip.astype(np.int64); kappa = (np.add.reduce(f.reshape(N, 8 * P), axis=1) & 31).reshape(N, 1, 1, 1)
        place = np.add.accumulate(f, axis=2) - 1; go = flip & (place < CAP)
        qb = np.take_along_axis(q, best[:, :, None, None, :], 3)[:, :, :, 0]; ub = np.take_along_axis(u, best[:, :, None, :], 2)[:, :, 0]
        new = X.copy()
        for r in range(N):
            d = (r + 1 + t % (N - 1)) % N
            for v in range(8):
                i = np.flatnonzero(go[r, v]); col = BL * place[r, v, i] + (ub[r, v, i] & (BL - 1))
                new[d, v][:, col] = (X[d, v][:, col] + qb[r, v][:, i]) >> 1
        X = new
    return {"yx": X.reshape(N, 128, W).astype(np.float32).astype(BF), "yl": E.reshape(N, 128, A).astype(np.float32), "ym": M.reshape(N, 128, A).astype(np.float32).astype(BF)}

@@ -1,0 +1,529 @@
+import numpy as np
+from concourse.mybir import AluOpType as ALU, AxisListType, ActivationFunctionType as ACT
+
+NX, NOFF, ZC, C15, TRO, WEND = 4096, 4096, 8192, 8193, 8208, 16400
+GW = 8208
+NENG = 8
+
+SCRATCH = {
+    "XT": ("sbuf", [128, WEND], "bfloat16"),
+    "ledI": ("sbuf", [128, 256], "int32"),
+    "E": ("sbuf", [128, 256], "float32"),
+    "Ek": ("sbuf", [128, 256], "float32"),
+    "mB": ("sbuf", [128, 256], "bfloat16"),
+    "sg": ("sbuf", [128, 256], "bfloat16"),
+    "LA": ("sbuf", [128, 256], "uint16"),
+    "LB": ("sbuf", [128, 256], "uint16"),
+    "LY": ("sbuf", [128, 256], "uint16"),
+    "tE": ("sbuf", [128, 256], "float32"),
+    "tM": ("sbuf", [128, 256], "float32"),
+    "dh": ("sbuf", [128, 256], "float32"),
+    "wE": ("sbuf", [128, 256], "float32"),
+    "wM": ("sbuf", [128, 256], "bfloat16"),
+    "Ab": ("sbuf", [128, 4096], "bfloat16"),
+    "Bb": ("sbuf", [128, 4096], "bfloat16"),
+    "bb": ("sbuf", [128, 4096 + 32], "bfloat16"),
+    "Qb": ("sbuf", [128, 4096 + 16], "bfloat16"),
+    "zb": ("sbuf", [128, 4096], "bfloat16"),
+    "sb": ("sbuf", [128, 4096], "bfloat16"),
+    "pb": ("sbuf", [128, 4096], "bfloat16"),
+    "zero": ("sbuf", [128, 1024], "bfloat16"),
+    "uI": ("sbuf", [128, 256], "int32"),
+    "uA": ("sbuf", [128, 256], "int32"),
+    "eu": ("sbuf", [128, 256], "int32"),
+    "wv": ("sbuf", [128, 256], "int32"),
+    "hs": ("sbuf", [128, 256], "int32"),
+    "hI": ("sbuf", [128, 256], "int32"),
+    "ov": ("sbuf", [128, 256], "bfloat16"),
+    "gov": ("sbuf", [128, 256], "bfloat16"),
+    "comp": ("sbuf", [128, 256], "float32"),
+    "R1": ("sbuf", [128, 256], "float32"),
+    "R2": ("sbuf", [128, 256], "float32"),
+    "win": ("sbuf", [128, 256], "bfloat16"),
+    "flipX": ("sbuf", [128, 256], "bfloat16"),
+    "wsb": ("sbuf", [128, 256], "bfloat16"),
+    "D": ("sbuf", [128, 1024], "float16"),
+    "LJ": ("sbuf", [128, 4], "uint16"),
+    "kr": ("sbuf", [128, 1], "float32"),
+    "kri": ("sbuf", [128, 1], "int32"),
+    "krm": ("sbuf", [128, 1], "int32"),
+    "kap": ("sbuf", [128, 1], "float32"),
+    "qs0": ("sbuf", [128, 64], "bfloat16"),
+    "qs1": ("sbuf", [128, 64], "bfloat16"),
+    "qs2": ("sbuf", [128, 64], "bfloat16"),
+    "land0": ("sbuf", [128, 64], "bfloat16"),
+    "land1": ("sbuf", [128, 64], "bfloat16"),
+    "land2": ("sbuf", [128, 64], "bfloat16"),
+    "vi": ("sbuf", [128, 4], "int32"),
+    "vm": ("sbuf", [128, 4], "int32"),
+    "vinv": ("sbuf", [128, 4], "float32"),
+    "vbs": ("sbuf", [128, 4], "float32"),
+    "vid": ("sbuf", [128, 4], "float32"),
+    "LI": ("sbuf", [128, 8], "uint16"),
+    "tx": ("sbuf", [128, 64], "float32"),
+    "ND": ("sbuf", [128, 128], "int32"),
+    "pI": ("sbuf", [128, 1], "int32"),
+    "kI": ("sbuf", [128, 1], "int32"),
+    "parI": ("sbuf", [128, 1], "int32"),
+    "kcol": ("sbuf", [128, 1], "float32"),
+    "sgn": ("sbuf", [128, 1], "float32"),
+    "offY": ("sbuf", [128, 1], "float32"),
+    "oB": ("sbuf", [128, 1], "float32"),
+    "s2c": ("sbuf", [128, 1], "float32"),
+    "s3c": ("sbuf", [128, 1], "float32"),
+    "wcol": ("sbuf", [128, 1], "float32"),
+    "w256": ("sbuf", [128, 1], "float32"),
+    "k64": ("sbuf", [128, 1], "float32"),
+    "i8": ("sbuf", [128, 8], "int32"),
+    "i8s": ("sbuf", [128, 8], "int32"),
+    "blkO": ("sbuf", [128, 8], "bfloat16"),
+    "blkE": ("sbuf", [128, 8], "bfloat16"),
+    "wb8": ("sbuf", [128, 8], "float32"),
+    "iD": ("sbuf", [128, 128], "int32"),
+    "iG": ("sbuf", [128, 128], "int32"),
+    "iGs": ("sbuf", [128, 128], "int32"),
+    "iR": ("sbuf", [128, 128], "int32"),
+    "iB": ("sbuf", [128, 4], "int32"),
+    "iC": ("sbuf", [128, 4], "int32"),
+    "ident": ("sbuf", [128, 128], "bfloat16"),
+    "tri": ("sbuf", [128, 128], "bfloat16"),
+    "all16": ("sbuf", [128, 128], "bfloat16"),
+    "ones": ("sbuf", [128, 128], "bfloat16"),
+    "onesh": ("sbuf", [128, 128], "float16"),
+    "bones": ("sbuf", [128, 128], "bfloat16"),
+    "kmat": ("sbuf", [128, 128], "bfloat16"),
+    "Pd": ("sbuf", [128, 128], "bfloat16"),
+    "crow": ("sbuf", [128, 128], "bfloat16"),
+    "Ct": ("sbuf", [128, 128], "float32"),
+    "base": ("sbuf", [128, 4], "float32"),
+    "jc": ("sbuf", [128, 4], "float16"),
+    "ecb": ("sbuf", [128, 16], "bfloat16"),
+    "ec": ("sbuf", [128, 16], "float16"),
+    "sel": ("sbuf", [128, 2048], "bfloat16"),
+    "pU0": ("psum", [128, 512], "float32"),
+    "pU1": ("psum", [128, 512], "float32"),
+    "pOV": ("psum", [128, 512], "float32"),
+    "pS": ("psum", [128, 512], "float32"),
+    "pGK": ("psum", [128, 512], "float32"),
+    "pWN": ("psum", [128, 512], "float32"),
+    "pZ": ("psum", [128, 512], "float32"),
+    "pSM": ("psum", [128, 512], "float32"),
+}
+SEMAPHORES = (["cV", "cS", "cP", "cG", "sent"] + ["arr%d" % t for t in range(3)] + ["d%d" % i for i in range(24)])
+
+
+def rank_program(g, core, T, topo):
+    rank = T.rank_of(core)
+    if rank is None:
+        return
+    n_ranks = len(T.cores)
+    rounds = 3
+    Q = {"V": g.vector, "S": g.scalar, "P": g.tensor, "G": g, "Y": g.sync}
+    count = {}
+    known = {q: {} for q in Q}
+    lastw, readers, banks = {}, {}, {}
+    seq = [0]
+    nd = [0]
+
+    def depends(q, R, W, B):
+        toks = []
+        for t in R:
+            if t in lastw:
+                toks.append(lastw[t])
+        for t in W:
+            if t in lastw:
+                toks.append(lastw[t])
+            toks += [x for x in readers.get(t, []) if x[2] != q]
+        for b in B:
+            toks += [x for qq, x in banks.get(b, {}).items() if qq != q]
+        for tok in sorted(toks, key=lambda x: -x[4]):
+            sem, val, _, snap, _ = tok
+            k = known[q]
+            if k.get(sem, 0) >= val:
+                continue
+            Q[q].wait_ge(T.sem[sem], val)
+            for s, v in snap.items():
+                if k.get(s, 0) < v:
+                    k[s] = v
+            k[sem] = max(k.get(sem, 0), val)
+
+    def note(q, sem, n, R, W, B):
+        count[sem] = count.get(sem, 0) + n
+        seq[0] += 1
+        tok = (sem, count[sem], q, dict(known[q]), seq[0])
+        for t in R:
+            readers.setdefault(t, []).append(tok)
+        for t in W:
+            lastw[t] = tok
+            readers[t] = []
+        for b in B:
+            banks.setdefault(b, {})[q] = tok
+        return tok
+
+    def op(q, f, R, W, B=()):
+        depends(q, R, W, B)
+        sem = "c" + q
+        f().then_inc(T.sem[sem], 1)
+        note(q, sem, 1, R, W, B)
+
+    def dma(q, out, in_, R, W):
+        depends(q, R, W, ())
+        sem = "d%d" % nd[0]
+        nd[0] += 1
+        Q[q].dma_start(out, in_).then_inc(T.sem[sem], 16)
+        note(q, sem, 16, R, W, ())
+
+    V, S, P = g.vector, g.scalar, g.tensor
+
+    def ts(out, in0, s1, s2, o0, o1=None):
+        if o1 is None:
+            return V.tensor_scalar(out, in0, s1, None, o0)
+        return V.tensor_scalar(out, in0, s1, s2, o0, o1)
+
+    def vts(out, in0, s1, o0, s2, o1, R, W, B=()):
+        op("V", lambda: ts(out, in0, s1, s2, o0, o1), R, W, B)
+
+    def vtt(out, a, b, o, R, W, B=()):
+        op("V", lambda: V.tensor_tensor(out, a, b, o), R, W, B)
+
+    def vcp(out, in_, R, W, B=()):
+        op("V", lambda: V.tensor_copy(out, in_), R, W, B)
+
+    def vms(ap, c, W):
+        op("V", lambda: V.memset(ap, c), [], W)
+
+    def sact(out, in_, f, R, W, B=(), bias=0.0, scale=1.0):
+        op("S", lambda: S.activation(out, in_, f, bias=bias, scale=scale), R, W, B)
+
+    def iota(out, pat, base, cm, W):
+        op("G", lambda: g.iota(out, pat, base, cm), [], W)
+
+    dma("S", T.ledI[:], T.led[:], [], ["ledI"])
+    for b in range(4):
+        c = slice(b * 1024, (b + 1) * 1024)
+        dma("Y", T.XT[:, c], T.xt[:, c], [], ["X%d" % b])
+        if b == 0:
+            dma("S", T.mB[:], T.mk[:], [], ["mB0", "mB1"])
+    XALL = ["X0", "X1", "X2", "X3", "N0", "N1", "N2", "N3", "C"]
+
+    iota(T.pI[:], [[0, 1]], 0, 1, ["pI"])
+    iota(T.i8[:], [[-16, 8]], 0, 1, ["i8"])
+    vms(T.ones[:], 1.0, ["ones"])
+    vts(T.kI[:], T.pI[:], 15, ALU.bitwise_and, None, None, ["pI"], ["kI"])
+    vts(T.i8s[:], T.i8[:], 4, ALU.arith_shift_right, None, None, ["i8"], ["i8s"])
+    vts(T.parI[:], T.kI[:], 1, ALU.bitwise_and, None, None, ["kI"], ["parI"])
+    vcp(T.kcol[:], T.kI[:], ["kI"], ["kcol"])
+    vts(T.blkO[:], T.i8s[:], 0, ALU.is_equal, None, None, ["i8s"], ["blkO"])
+    vts(T.wcol[:], T.kI[:], 2.0, ALU.mult, 1.0, ALU.add, ["kI"], ["wcol"])
+    vts(T.offY[:], T.parI[:], -float(NOFF), ALU.mult, float(NOFF), ALU.add, ["parI"], ["offY"])
+    vts(T.oB[:], T.parI[:], float(NOFF), ALU.mult, -float(ZC), ALU.add, ["parI"], ["oB"])
+    vts(T.wb8[:], T.blkO[:], T.wcol[:, 0:1], ALU.mult, None, None, ["blkO", "wcol"], ["wb8"])
+    vts(T.s2c[:], T.kcol[:], 14.5, ALU.is_lt, None, None, ["kcol"], ["s2c"])
+    vts(T.s3c[:], T.kcol[:], 14.5, ALU.is_ge, float(ZC), ALU.add, ["kcol"], ["s3c"])
+    vms(T.sel[:], 0.0, ["sel"])
+    vms(T.XT[:, ZC:ZC + 16], 0.0, ["C"])
+    vms(T.XT[:, C15:C15 + 1], -2048.0, ["C"])
+    vms(T.zero[:], 0.0, ["zero"])
+    vms(T.bb[:, 0:16], 0.0, ["bbx"])
+    for b in range(8):
+        sact(T.sel[:, 16 * b:16 * b + 129 * 15 + 1:129], T.ones[:, 0:16], ACT.Copy, ["ones", "wb8", "sel"] if b == 0 else
+             ["ones", "wb8"], ["selg%d" % b], scale=T.wb8[:, b:b + 1])
+    SEL = ["sel"] + ["selg%d" % b for b in range(8)]
+    iota(T.iD[:], [[1, 128]], 0, -1, ["iD"])
+    iota(T.iG[:], [[-16, 8], [0, 16]], 0, 1, ["iG"])
+    iota(T.iR[:], [[0, 8], [1, 16]], 0, 0, ["iR"])
+    iota(T.iB[:], [[1024, 4]], 0, 0, ["iB"])
+    iota(T.iC[:], [[512, 4]], 32, 0, ["iC"])
+
+    def lists(hs_):
+        vts(T.LA[:, hs_], T.E[:, hs_], T.offY[:, 0:1], ALU.add, None, None, ["E0", "E1", "offY"], ["LA"])
+        vts(T.tE[:, hs_], T.E[:, hs_], T.oB[:, 0:1], ALU.add, None, None, ["E0", "E1", "oB"], ["tE"])
+        vtt(T.tM[:, hs_], T.tE[:, hs_], T.mB[:, hs_], ALU.mult, ["tE", "mB0", "mB1"], ["tM"])
+        vts(T.LB[:, hs_], T.tM[:, hs_], T.s2c[:, 0:1], ALU.mult, T.s3c[:, 0:1], ALU.add, ["tM", "s2c", "s3c"], ["LB"])
+
+    full = slice(0, 256)
+    vcp(T.E[:], T.ledI[:], ["ledI"], ["E0", "E1"])
+    lists(full)
+    vts(T.sg[:], T.mB[:], -2.0, ALU.mult, 1.0, ALU.add, ["mB0", "mB1"], ["sg0", "sg1"])
+    vts(T.sgn[:], T.parI[:], 2.0, ALU.mult, -1.0, ALU.add, ["parI"], ["sgn"])
+    for b in range(4):
+        c = slice(b * 1024, (b + 1) * 1024)
+        cn = slice(NOFF + b * 1024, NOFF + (b + 1) * 1024)
+        if b % 2 == 0:
+            vts(T.XT[:, cn], T.XT[:, c], -1.0, ALU.mult, None, None, ["X%d" % b], ["N%d" % b])
+        else:
+            sact(T.XT[:, cn], T.XT[:, c], ACT.Copy, ["X%d" % b], ["N%d" % b], scale=-1.0)
+
+    def late_constants():
+        vts(T.w256[:], T.kcol[:], -1.0, ALU.mult, 256.0, ALU.add, ["kcol"], ["w256"])
+        vts(T.k64[:], T.kcol[:], 64.0, ALU.mult, None, None, ["kcol"], ["k64"])
+        vts(T.blkE[:], T.blkO[:], -1.0, ALU.mult, None, None, ["blkO"], ["blkE"])
+        vts(T.ident[:], T.iD[:], 0, ALU.is_equal, None, None, ["iD"], ["ident"])
+        vts(T.tri[:], T.iD[:], 0, ALU.is_ge, -16.0, ALU.mult, ["iD"], ["tri"])
+        vts(T.iGs[:], T.iG[:], 4, ALU.arith_shift_right, None, None, ["iG"], ["iGs"])
+        vts(T.crow[:], T.iR[:], 0.125, ALU.mult, None, None, ["iR"], ["crow"])
+        vts(T.Pd[:], T.ident[:], T.w256[:, 0:1], ALU.mult, None, None, ["ident", "w256"], ["Pd"])
+        vts(T.kmat[:], T.iGs[:], 0, ALU.is_equal, T.kcol[:, 0:1], ALU.mult, ["iGs", "kcol"], ["kmat"])
+        vts(T.base[:], T.iB[:], T.k64[:, 0:1], ALU.add, None, None, ["iB", "k64"], ["base"])
+        vcp(T.jc[:], T.iC[:], ["iC"], ["jc"])
+        vms(T.all16[:], -16.0, ["all16"])
+        vms(T.ecb[:], 0.0, ["ecb"])
+        vms(T.ecb[:, 0:16:5], 1.0, ["ecb"])
+        vcp(T.ec[:], T.ecb[:], ["ecb"], ["ec"])
+        vcp(T.onesh[:], T.ones[:], ["ones"], ["onesh"])
+        vms(T.Ct[:], 16384.0, ["Ct"])
+        vms(T.Ct[:, 0:128:16], 0.5, ["Ct"])
+        vms(T.Qb[:, 4096:4112], 256.0, ["Qx"])
+
+    def trash_fill():
+        vms(T.XT[:, TRO:TRO + 4096], 0.0, ["T1"])
+
+    def ce(i):
+        return slice(i * 1024, (i + 1) * 1024)
+
+    def ca(i):
+        return slice(i * 64, (i + 1) * 64)
+
+    def cb(b):
+        return slice(b * 128, (b + 1) * 128)
+
+    def gather(q, out, lst, i, R, W):
+        src = T.XT[:, 0:GW].indirect(lst[:, ca(i)])
+        if q == "V":
+            vcp(out[:, ce(i)], src, R + XALL, W)
+        else:
+            sact(out[:, ce(i)], src, ACT.Copy, R + XALL, W)
+
+    def gA(q, i):
+        gather(q, T.Ab, T.LA, i, ["LA"], ["A%d" % i])
+
+    def gB(q, i):
+        gather(q, T.Bb, T.LB, i, ["LB"], ["B%d" % i])
+
+    def scans(i):
+        o = slice(i * 1024 + 16, (i + 1) * 1024 + 16)
+        op("V", lambda: V.tensor_tensor_scan(T.bb[:, o], T.Bb[:, ce(i)], T.zero[:], 0.0, ALU.add, ALU.max),
+           ["B%d" % i, "zero"], ["bb%d" % i])
+        p = slice(i * 1024 + 15, (i + 1) * 1024 + 15)
+        op("V", lambda: V.tensor_tensor_scan(T.Qb[:, ce(i)], T.bb[:, p], T.Ab[:, ce(i)], 0.0, ALU.max, ALU.min),
+           ["bb%d" % i, "bbx" if i == 0 else "bb%d" % (i - 1), "A%d" % i], ["Q%d" % i])
+
+    def over(q, i):
+        if q == "V":
+            vts(T.pb[:, ce(i)], T.Qb[:, ce(i)], -1.0, ALU.max, 1.0, ALU.min, ["Q%d" % i], ["p%d" % i])
+        else:
+            sact(T.pb[:, ce(i)], T.Qb[:, ce(i)], ACT.Sign, ["Q%d" % i], ["p%d" % i])
+
+    def group(calls, R, W, B):
+        def f():
+            r = None
+            for c in calls:
+                r = P.matmul(*c)
+            return r
+        op("P", f, R, W, B)
+
+    def pU(i):
+        n = "pU%d" % (i % 2)
+        group([(T[n][:, 0:64], T.sel[:, 128 * k:128 * (k + 1)], T.Qb[:, i * 1024 + k:(i + 1) * 1024:16], k == 0, k == 15)
+               for k in range(16)], SEL + ["Q%d" % i], [n], [n])
+
+    def hchain(i, t):
+        n = "pU%d" % (i % 2)
+        a = ca(i)
+        s = str(i)
+        e = "E%d" % (i // 2)
+        vts(T.uI[:, a], T[n][:, 0:64], T.sgn[:, 0:1], ALU.mult, None, None, [n, "sgn"], ["uI" + s], [n])
+        vts(T.uA[:, a], T.uI[:, a], 4095, ALU.bitwise_and, None, None, ["uI" + s], ["uA" + s])
+        vtt(T.eu[:, a], T.E[:, a], T.uA[:, a], ALU.mult, ["uA" + s, e], ["eu" + s])
+        vts(T.wv[:, a], T.eu[:, a], 5, ALU.arith_shift_right, 4095, ALU.bitwise_and, ["eu" + s], ["wv" + s])
+        ek = T.E if t == 0 else T.Ek
+        vtt(T.hs[:, a], T.wv[:, a], ek[:, a], ALU.add, ["wv" + s, e if t == 0 else "Ek"], ["hs" + s])
+        vts(T.hI[:, a], T.hs[:, a], 4095, ALU.bitwise_and, None, None, ["hs" + s], ["hI" + s])
+        vts(T.LY[:, a], T.hI[:, a], T.offY[:, 0:1], ALU.add, None, None, ["hI" + s, "offY"], ["LY" + s])
+
+    def ysub(i):
+        vtt(T.zb[:, ce(i)], T.XT[:, 0:GW].indirect(T.LY[:, ca(i)]), T.Qb[:, ce(i)], ALU.subtract,
+            ["LY%d" % i, "Q%d" % i] + XALL, ["z%d" % i])
+
+    def sign(q, i):
+        if q == "V":
+            vts(T.sb[:, ce(i)], T.zb[:, ce(i)], -1.0, ALU.max, 1.0, ALU.min, ["z%d" % i], ["s%d" % i])
+        else:
+            sact(T.sb[:, ce(i)], T.zb[:, ce(i)], ACT.Sign, ["z%d" % i], ["s%d" % i])
+
+    def sums(ps, src, tag, b):
+        group([(T[ps][:, b * 128 + k:(b + 1) * 128:16], src[:, b * 2048 + k:(b + 1) * 2048:16],
+                (T.blkE if k % 2 == 0 else T.blkO)[:], True, True) for k in range(16)],
+              [tag + str(2 * b), tag + str(2 * b + 1), "blkE", "blkO"], [ps + str(b)], [ps])
+
+    def pGK():
+        group([(T.pGK[:, cb(b)], T.sg[:, cb(b)], T.Pd[:], True, True) for b in range(2)], ["sg0", "sg1", "Pd"], ["pGK"], ["pGK"])
+
+    def dec_over(b):
+        s = str(b)
+        vts(T.ov[:, cb(b)], T.pOV[:, cb(b)], 8.5, ALU.is_ge, None, None, ["pOV" + s], ["ov" + s], ["pOV"])
+        vtt(T.gov[:, cb(b)], T.pGK[:, cb(b)], T.ov[:, cb(b)], ALU.mult, ["pGK", "ov" + s], ["gov" + s], ["pGK"])
+
+    def decide(b):
+        s = str(b)
+        c = cb(b)
+        vtt(T.comp[:, c], T.pS[:, c], T.gov[:, c], ALU.mult, ["pS" + s, "gov" + s], ["comp" + s], ["pS"])
+        op("V", lambda: V.tensor_tensor_scan(T.R1[:, c], T.Ct[:], T.comp[:, c], 0.5, ALU.min, ALU.max), ["Ct", "comp" + s],
+           ["R1" + s])
+        vcp(T.R1[:, b * 128:(b + 1) * 128:16], T.R1[:, b * 128 + 15:(b + 1) * 128:16], ["R1" + s], ["R1" + s])
+        op("V", lambda: V.tensor_tensor_scan(T.R2[:, c], T.Ct[:], T.R1[:, c], 0.5, ALU.min, ALU.max), ["Ct", "R1" + s],
+           ["R2" + s])
+        vtt(T.win[:, c], T.comp[:, c], T.R2[:, c], ALU.is_equal, ["comp" + s, "R2" + s], ["win" + s])
+        sact(T.flipX[:, c], T.R2[:, c], ACT.Sign, ["R2" + s, "half"], ["fl" + s], bias=T.Ct[:, 0:1] if False else -0.5)
+        group([(T.pWN[:, c], T.win[:, c], T.ident[:], True, True)], ["win" + s, "ident"], ["pWN" + s], ["pWN"])
+        calls = [(T.pZ[:, c], T.tri[:], T.flipX[:, c], True, False), (T.pZ[:, c], T.ones[:], T.crow[:], False, False)]
+        R = ["tri", "fl" + s, "ones", "crow"]
+        if b == 1:
+            calls.append((T.pZ[:, c], T.all16[:], T.flipX[:, cb(0)], False, False))
+            R += ["all16", "fl0"]
+        group(calls, R, ["pZ" + s], ["pZ"])
+        sact(T.wsb[:, c], T.pWN[:, c], ACT.Copy, ["pWN" + s], ["wsb" + s], ["pWN"])
+        group([(T.pZ[:, c], T.wsb[:, c], T.kmat[:], False, True)], ["wsb" + s, "kmat"], ["pZ" + s], ["pZ"])
+
+    def clamps(b):
+        s = str(b)
+        for c in range(4):
+            lo = -(256.0 * c + 16)
+            o = slice(c * 256 + b * 128, c * 256 + (b + 1) * 128)
+            vts(T.D[:, o], T.pZ[:, cb(b)], lo, ALU.max, lo + 16, ALU.min, ["pZ" + s], ["D%d%d" % (c, b)], ["pZ"])
+
+    def pLJ():
+        calls = [(T.pSM[:, 0:4], T.onesh[:], T.jc[:], True, False)]
+        for b in range(2):
+            for c in range(4):
+                calls.append((T.pSM[:, 0:4], T.D[:, c * 256 + b * 128:c * 256 + (b + 1) * 128], T.ec[:, 4 * c:4 * c + 4], False,
+                              b == 1 and c == 3))
+        group(calls, ["onesh", "jc", "ec"] + ["D%d%d" % (c, b) for c in range(4) for b in range(2)], ["LJp"], ["pSM"])
+
+    def send(t):
+        vcp(T.LJ[:], T.pSM[:, 0:4], ["LJp"], ["LJ"], ["pSM"])
+        qn = "qs%d" % t
+        sact(T[qn][:], T.Qb[:].indirect(T.LJ[:, 0:4]), ACT.Abs, ["LJ", "Qx", "Q0", "Q1", "Q2", "Q3"], [qn])
+        dst = T.cores[(rank + 1 + t % (n_ranks - 1)) % n_ranks]
+        rid, pid, _ = topo.addr(dst)
+        eng = topo.engines(core, dst)[:NENG]
+        depends("G", [qn], [], ())
+        g.remote_dma(T["land%d" % t][:], T[qn][:], T.sem["arr%d" % t], T.sem.sent, pid, rid, sum(1 << e for e in eng))
+        count["sent"] = count.get("sent", 0) + len(eng)
+        src = T.cores[(rank - 1 - t % (n_ranks - 1)) % n_ranks]
+        note("R", "arr%d" % t, len(topo.engines(src, core)[:NENG]), [], ["land%d" % t], ())
+
+    known["R"] = {}
+
+    def kappa():
+        group([(T.pSM[:, 16:24], T.ones[:], T.flipX[:, b * 128:(b + 1) * 128:16], b == 0, b == 1) for b in range(2)],
+              ["ones", "fl0", "fl1"], ["kp"], ["pSM"])
+
+    def kappa2():
+        op("V", lambda: V.tensor_reduce(T.kr[:], T.pSM[:, 16:24], AxisListType.X, ALU.add), ["kp"], ["kr"], ["pSM"])
+        vcp(T.kri[:], T.kr[:], ["kr"], ["kri"])
+
+    def update(last):
+        for b in range(2):
+            c = cb(b)
+            s = str(b)
+            vtt(T.dh[:, c], T.hI[:, c], T.E[:, c], ALU.subtract, ["hI%d" % (2 * b), "hI%d" % (2 * b + 1), "E" + s], ["dh" + s])
+            vtt(T.wM[:, c], T.pWN[:, c], T.sg[:, c], ALU.mult, ["pWN" + s, "sg" + s], ["wM" + s], ["pWN"])
+            vtt(T.wE[:, c], T.pWN[:, c], T.dh[:, c], ALU.mult, ["pWN" + s, "dh" + s], ["wE" + s], ["pWN"])
+            vtt(T.mB[:, c], T.mB[:, c], T.wM[:, c], ALU.add, ["mB" + s, "wM" + s], ["mB" + s])
+            vtt(T.E[:, c], T.E[:, c], T.wE[:, c], ALU.add, ["E" + s, "wE" + s], ["E" + s])
+        if last:
+            dma("Y", T.ym[:], T.mB[:], ["mB0", "mB1"], ["ym"])
+            dma("S", T.yl[:], T.E[:], ["E0", "E1"], ["yl"])
+            return
+        vts(T.krm[:], T.kri[:], 31, ALU.bitwise_and, None, None, ["kri"], ["krm"])
+        lists(full)
+        vts(T.sg[:], T.mB[:], -2.0, ALU.mult, 1.0, ALU.add, ["mB0", "mB1"], ["sg0", "sg1"])
+        vcp(T.kap[:], T.krm[:], ["krm"], ["kap"])
+        vts(T.Ek[:], T.E[:], T.kap[:, 0:1], ALU.add, None, None, ["E0", "E1", "kap"], ["Ek"])
+        pGK()
+
+    def arrive(t, last):
+        ln = "land%d" % t
+        group([(T.pSM[:, 32:36], T.sel[:, 128 * r:128 * (r + 1)], T[ln][:, r:64:16], r == 0, r == 15) for r in range(16)],
+              SEL + [ln], ["pA"], ["pSM"])
+        vcp(T.vi[:], T.pSM[:, 32:36], ["pA"], ["vi"], ["pSM"])
+        vts(T.vinv[:], T.pSM[:, 32:36], 65535.5, ALU.is_ge, float(TRO), ALU.mult, ["pA"], ["vinv"], ["pSM"])
+        vts(T.vm[:], T.vi[:], 63, ALU.bitwise_and, None, None, ["vi"], ["vm"])
+        vtt(T.vbs[:], T.vinv[:], T.base[:], ALU.add, ["vinv", "base"], ["vbs"])
+        vtt(T.vid[:], T.vm[:], T.vbs[:], ALU.add, ["vm", "vbs"], ["vid"])
+        vcp(T.LI[:, 0:4], T.vid[:], ["vid"], ["LI"])
+        vts(T.LI[:, 4:8], T.vid[:], float(NOFF), ALU.add, None, None, ["vid"], ["LI2"])
+        vtt(T.tx[:], T.XT[:, 0:TRO + 4096].indirect(T.LI[:, 0:4]), T[ln][:], ALU.add, ["LI", ln, "T1"] + XALL, ["tx"])
+        vts(T.ND[:, 0:64], T.tx[:], 0.5, ALU.mult, -0.25, ALU.add, ["tx"], ["ND0"])
+        xw = XALL[:8] + ["T1"]
+        if last:
+            op("V", lambda: V.tensor_copy(T.XT[:, 0:WEND].indirect(T.LI[:, 0:4]), T.ND[:, 0:64]), ["LI", "ND0"], xw)
+        else:
+            vts(T.ND[:, 64:128], T.tx[:], -0.5, ALU.mult, 0.25, ALU.add, ["tx"], ["ND1"])
+            op("V", lambda: V.tensor_copy(T.XT[:, 0:WEND].indirect(T.LI[:, 0:8]), T.ND[:]), ["LI", "LI2", "ND0", "ND1"],
+               xw + ["C"])
+
+    for t in range(rounds):
+        last = t == rounds - 1
+        gA("V", 0)
+        gB("S", 0)
+        gA("S", 1)
+        gB("S", 1)
+        if t == 0:
+            late_constants()
+            pGK()
+        scans(0)
+        pU(0)
+        over("V", 0)
+        gA("S", 2)
+        gB("S", 2)
+        hchain(0, t)
+        ysub(0)
+        scans(1)
+        pU(1)
+        over("V", 1)
+        sums("pOV", T.pb, "p", 0)
+        sign("S", 0)
+        gA("S", 3)
+        gB("S", 3)
+        hchain(1, t)
+        scans(2)
+        pU(2)
+        ysub(1)
+        sign("S", 1)
+        over("S", 2)
+        sums("pS", T.sb, "s", 0)
+        hchain(2, t)
+        scans(3)
+        pU(3)
+        ysub(2)
+        sign("S", 2)
+        over("S", 3)
+        sums("pOV", T.pb, "p", 1)
+        dec_over(0)
+        decide(0)
+        hchain(3, t)
+        ysub(3)
+        sign("V", 3)
+        sums("pS", T.sb, "s", 1)
+        clamps(0)
+        dec_over(1)
+        if t == 0:
+            trash_fill()
+        decide(1)
+        clamps(1)
+        pLJ()
+        if not last:
+            kappa()
+        send(t)
+        if not last:
+            kappa2()
+        update(last)
+        arrive(t, last)
+    for b in range(4):
+        c = slice(b * 1024, (b + 1) * 1024)
+        dma("Y" if b % 2 == 0 else "S", T.yx[:, c], T.XT[:, c], ["X%d" % b], ["yx%d" % b])
+    for sem, n in count.items():
+        if known["G"].get(sem, 0) < n:
+            g.wait_ge(T.sem[sem], n)

@@ -90,7 +90,6 @@ SCRATCH = {
     "all16": ("sbuf", [128, 128], "bfloat16"),
     "ones": ("sbuf", [128, 128], "bfloat16"),
     "onesh": ("sbuf", [128, 128], "float16"),
-    "bones": ("sbuf", [128, 128], "bfloat16"),
     "kmat": ("sbuf", [128, 128], "bfloat16"),
     "Pd": ("sbuf", [128, 128], "bfloat16"),
     "crow": ("sbuf", [128, 128], "bfloat16"),
@@ -118,12 +117,12 @@ def rank_program(g, core, T, topo):
         return
     n_ranks = len(T.cores)
     rounds = 3
-    Q = {"V": g.vector, "S": g.scalar, "P": g.tensor, "G": g, "Y": g.sync}
+    V, S, P = g.vector, g.scalar, g.tensor
+    Q = {"V": V, "S": S, "P": P, "G": g, "Y": g.sync}
     count = {}
     known = {q: {} for q in Q}
     lastw, readers, banks = {}, {}, {}
-    seq = [0]
-    nd = [0]
+    seq, nd = [0], [0]
 
     def depends(q, R, W, B):
         toks = []
@@ -136,8 +135,7 @@ def rank_program(g, core, T, topo):
             toks += [x for x in readers.get(t, []) if x[2] != q]
         for b in B:
             toks += [x for qq, x in banks.get(b, {}).items() if qq != q]
-        for tok in sorted(toks, key=lambda x: -x[4]):
-            sem, val, _, snap, _ = tok
+        for sem, val, _, snap, _ in sorted(toks, key=lambda x: -x[4]):
             k = known[q]
             if k.get(sem, 0) >= val:
                 continue
@@ -147,10 +145,10 @@ def rank_program(g, core, T, topo):
                     k[s] = v
             k[sem] = max(k.get(sem, 0), val)
 
-    def note(q, sem, n, R, W, B):
+    def note(q, sem, n, R, W, B, snap):
         count[sem] = count.get(sem, 0) + n
         seq[0] += 1
-        tok = (sem, count[sem], q, dict(known[q]), seq[0])
+        tok = (sem, count[sem], q, snap, seq[0])
         for t in R:
             readers.setdefault(t, []).append(tok)
         for t in W:
@@ -158,30 +156,24 @@ def rank_program(g, core, T, topo):
             readers[t] = []
         for b in B:
             banks.setdefault(b, {})[q] = tok
-        return tok
 
     def op(q, f, R, W, B=()):
         depends(q, R, W, B)
-        sem = "c" + q
-        f().then_inc(T.sem[sem], 1)
-        note(q, sem, 1, R, W, B)
+        f().then_inc(T.sem["c" + q], 1)
+        note(q, "c" + q, 1, R, W, B, dict(known[q]))
 
     def dma(q, out, in_, R, W):
         depends(q, R, W, ())
         sem = "d%d" % nd[0]
         nd[0] += 1
         Q[q].dma_start(out, in_).then_inc(T.sem[sem], 16)
-        note(q, sem, 16, R, W, ())
-
-    V, S, P = g.vector, g.scalar, g.tensor
-
-    def ts(out, in0, s1, s2, o0, o1=None):
-        if o1 is None:
-            return V.tensor_scalar(out, in0, s1, None, o0)
-        return V.tensor_scalar(out, in0, s1, s2, o0, o1)
+        note(q, sem, 16, R, W, (), dict(known[q]))
 
     def vts(out, in0, s1, o0, s2, o1, R, W, B=()):
-        op("V", lambda: ts(out, in0, s1, s2, o0, o1), R, W, B)
+        if o1 is None:
+            op("V", lambda: V.tensor_scalar(out, in0, s1, None, o0), R, W, B)
+        else:
+            op("V", lambda: V.tensor_scalar(out, in0, s1, s2, o0, o1), R, W, B)
 
     def vtt(out, a, b, o, R, W, B=()):
         op("V", lambda: V.tensor_tensor(out, a, b, o), R, W, B)
@@ -195,8 +187,18 @@ def rank_program(g, core, T, topo):
     def sact(out, in_, f, R, W, B=(), bias=0.0, scale=1.0):
         op("S", lambda: S.activation(out, in_, f, bias=bias, scale=scale), R, W, B)
 
-    def iota(out, pat, base, cm, W):
-        op("G", lambda: g.iota(out, pat, base, cm), [], W)
+    def iota(out, pat, base, cm, W, small=False):
+        if small:
+            op("G", lambda: g.iota(out, pat, base, cm, allow_small_or_imprecise_dtypes=True), [], W)
+        else:
+            op("G", lambda: g.iota(out, pat, base, cm), [], W)
+
+    def do(*lists_):
+        lists_ = [list(x) for x in lists_ if x]
+        while lists_:
+            for x in lists_:
+                x.pop(0)()
+            lists_ = [x for x in lists_ if x]
 
     dma("S", T.ledI[:], T.led[:], [], ["ledI"])
     for b in range(4):
@@ -204,11 +206,12 @@ def rank_program(g, core, T, topo):
         dma("Y", T.XT[:, c], T.xt[:, c], [], ["X%d" % b])
         if b == 0:
             dma("S", T.mB[:], T.mk[:], [], ["mB0", "mB1"])
-    XALL = ["X0", "X1", "X2", "X3", "N0", "N1", "N2", "N3", "C"]
+    XALL = ["X0", "X1", "X2", "X3", "N0", "N1", "N2", "N3", "N1s", "N3s", "C"]
 
     iota(T.pI[:], [[0, 1]], 0, 1, ["pI"])
     iota(T.i8[:], [[-16, 8]], 0, 1, ["i8"])
     vms(T.ones[:], 1.0, ["ones"])
+    vms(T.sel[:], 0.0, ["sel"])
     vts(T.kI[:], T.pI[:], 15, ALU.bitwise_and, None, None, ["pI"], ["kI"])
     vts(T.i8s[:], T.i8[:], 4, ALU.arith_shift_right, None, None, ["i8"], ["i8s"])
     vts(T.parI[:], T.kI[:], 1, ALU.bitwise_and, None, None, ["kI"], ["parI"])
@@ -220,63 +223,72 @@ def rank_program(g, core, T, topo):
     vts(T.wb8[:], T.blkO[:], T.wcol[:, 0:1], ALU.mult, None, None, ["blkO", "wcol"], ["wb8"])
     vts(T.s2c[:], T.kcol[:], 14.5, ALU.is_lt, None, None, ["kcol"], ["s2c"])
     vts(T.s3c[:], T.kcol[:], 14.5, ALU.is_ge, float(ZC), ALU.add, ["kcol"], ["s3c"])
-    vms(T.sel[:], 0.0, ["sel"])
     vms(T.XT[:, ZC:ZC + 16], 0.0, ["C"])
-    vms(T.XT[:, C15:C15 + 1], -2048.0, ["C"])
     vms(T.zero[:], 0.0, ["zero"])
+    vms(T.XT[:, C15:C15 + 1], -2048.0, ["C"])
     vms(T.bb[:, 0:16], 0.0, ["bbx"])
     for b in range(8):
-        sact(T.sel[:, 16 * b:16 * b + 129 * 15 + 1:129], T.ones[:, 0:16], ACT.Copy, ["ones", "wb8", "sel"] if b == 0 else
-             ["ones", "wb8"], ["selg%d" % b], scale=T.wb8[:, b:b + 1])
+        sact(T.sel[:, 16 * b:16 * b + 129 * 15 + 1:129], T.ones[:, 0:16], ACT.Copy, ["ones", "wb8", "sel"], ["selg%d" % b],
+             scale=T.wb8[:, b:b + 1])
     SEL = ["sel"] + ["selg%d" % b for b in range(8)]
     iota(T.iD[:], [[1, 128]], 0, -1, ["iD"])
     iota(T.iG[:], [[-16, 8], [0, 16]], 0, 1, ["iG"])
     iota(T.iR[:], [[0, 8], [1, 16]], 0, 0, ["iR"])
     iota(T.iB[:], [[1024, 4]], 0, 0, ["iB"])
     iota(T.iC[:], [[512, 4]], 32, 0, ["iC"])
+    iota(T.Qb[:, 4096:4112], [[0, 16]], 256, 0, ["Qx"], True)
+    iota(T.XT[:, TRO:TRO + 4096], [[0, 4096]], 0, 0, ["T1"], True)
 
-    def lists(hs_):
-        vts(T.LA[:, hs_], T.E[:, hs_], T.offY[:, 0:1], ALU.add, None, None, ["E0", "E1", "offY"], ["LA"])
-        vts(T.tE[:, hs_], T.E[:, hs_], T.oB[:, 0:1], ALU.add, None, None, ["E0", "E1", "oB"], ["tE"])
-        vtt(T.tM[:, hs_], T.tE[:, hs_], T.mB[:, hs_], ALU.mult, ["tE", "mB0", "mB1"], ["tM"])
-        vts(T.LB[:, hs_], T.tM[:, hs_], T.s2c[:, 0:1], ALU.mult, T.s3c[:, 0:1], ALU.add, ["tM", "s2c", "s3c"], ["LB"])
+    def lists(c=slice(0, 256)):
+        return [
+            lambda: vts(T.LA[:, c], T.E[:, c], T.offY[:, 0:1], ALU.add, None, None, ["E0", "E1", "offY"], ["LA"]),
+            lambda: sact(T.tE[:, c], T.E[:, c], ACT.Identity, ["E0", "E1", "oB"], ["tE"], bias=T.oB[:, 0:1]),
+            lambda: vtt(T.tM[:, c], T.tE[:, c], T.mB[:, c], ALU.mult, ["tE", "mB0", "mB1"], ["tM"]),
+            lambda: vts(T.LB[:, c], T.tM[:, c], T.s2c[:, 0:1], ALU.mult, T.s3c[:, 0:1], ALU.add, ["tM", "s2c", "s3c"], ["LB"]),
+        ]
 
-    full = slice(0, 256)
-    vcp(T.E[:], T.ledI[:], ["ledI"], ["E0", "E1"])
-    lists(full)
-    vts(T.sg[:], T.mB[:], -2.0, ALU.mult, 1.0, ALU.add, ["mB0", "mB1"], ["sg0", "sg1"])
-    vts(T.sgn[:], T.parI[:], 2.0, ALU.mult, -1.0, ALU.add, ["parI"], ["sgn"])
-    for b in range(4):
-        c = slice(b * 1024, (b + 1) * 1024)
-        cn = slice(NOFF + b * 1024, NOFF + (b + 1) * 1024)
-        if b % 2 == 0:
+    def signs():
+        sact(T.sg[:], T.mB[:], ACT.Copy, ["mB0", "mB1"], ["sg0", "sg1"], bias=1.0, scale=-2.0)
+
+    def neg(q, b, lo=0, hi=1024):
+        c = slice(b * 1024 + lo, b * 1024 + hi)
+        cn = slice(NOFF + b * 1024 + lo, NOFF + b * 1024 + hi)
+        if q == "V":
             vts(T.XT[:, cn], T.XT[:, c], -1.0, ALU.mult, None, None, ["X%d" % b], ["N%d" % b])
         else:
-            sact(T.XT[:, cn], T.XT[:, c], ACT.Copy, ["X%d" % b], ["N%d" % b], scale=-1.0)
+            sact(T.XT[:, cn], T.XT[:, c], ACT.Copy, ["X%d" % b], ["N%ds" % b], scale=-1.0)
 
-    def late_constants():
-        vts(T.w256[:], T.kcol[:], -1.0, ALU.mult, 256.0, ALU.add, ["kcol"], ["w256"])
-        vts(T.k64[:], T.kcol[:], 64.0, ALU.mult, None, None, ["kcol"], ["k64"])
-        vts(T.blkE[:], T.blkO[:], -1.0, ALU.mult, None, None, ["blkO"], ["blkE"])
-        vts(T.ident[:], T.iD[:], 0, ALU.is_equal, None, None, ["iD"], ["ident"])
-        vts(T.tri[:], T.iD[:], 0, ALU.is_ge, -16.0, ALU.mult, ["iD"], ["tri"])
-        vts(T.iGs[:], T.iG[:], 4, ALU.arith_shift_right, None, None, ["iG"], ["iGs"])
-        vts(T.crow[:], T.iR[:], 0.125, ALU.mult, None, None, ["iR"], ["crow"])
-        vts(T.Pd[:], T.ident[:], T.w256[:, 0:1], ALU.mult, None, None, ["ident", "w256"], ["Pd"])
-        vts(T.kmat[:], T.iGs[:], 0, ALU.is_equal, T.kcol[:, 0:1], ALU.mult, ["iGs", "kcol"], ["kmat"])
-        vts(T.base[:], T.iB[:], T.k64[:, 0:1], ALU.add, None, None, ["iB", "k64"], ["base"])
-        vcp(T.jc[:], T.iC[:], ["iC"], ["jc"])
-        vms(T.all16[:], -16.0, ["all16"])
-        vms(T.ecb[:], 0.0, ["ecb"])
-        vms(T.ecb[:, 0:16:5], 1.0, ["ecb"])
-        vcp(T.ec[:], T.ecb[:], ["ecb"], ["ec"])
-        vcp(T.onesh[:], T.ones[:], ["ones"], ["onesh"])
-        vms(T.Ct[:], 16384.0, ["Ct"])
-        vms(T.Ct[:, 0:128:16], 0.5, ["Ct"])
-        vms(T.Qb[:, 4096:4112], 256.0, ["Qx"])
-
-    def trash_fill():
-        vms(T.XT[:, TRO:TRO + 4096], 0.0, ["T1"])
+    late = [
+        lambda: vts(T.w256[:], T.kcol[:], -1.0, ALU.mult, 256.0, ALU.add, ["kcol"], ["w256"]),
+        lambda: vts(T.ident[:], T.iD[:], 0, ALU.is_equal, None, None, ["iD"], ["ident"]),
+        lambda: vts(T.blkE[:], T.blkO[:], -1.0, ALU.mult, None, None, ["blkO"], ["blkE"]),
+        lambda: vts(T.iGs[:], T.iG[:], 4, ALU.arith_shift_right, None, None, ["iG"], ["iGs"]),
+        lambda: vts(T.Pd[:], T.ident[:], T.w256[:, 0:1], ALU.mult, None, None, ["ident", "w256"], ["Pd"]),
+        lambda: vts(T.tri[:], T.iD[:], 0, ALU.is_ge, -16.0, ALU.mult, ["iD"], ["tri"]),
+        lambda: vts(T.kmat[:], T.iGs[:], 0, ALU.is_equal, T.kcol[:, 0:1], ALU.mult, ["iGs", "kcol"], ["kmat"]),
+        lambda: vts(T.crow[:], T.iR[:], 0.125, ALU.mult, None, None, ["iR"], ["crow"]),
+        lambda: vms(T.Ct[:], 16384.0, ["Ct"]),
+        lambda: vms(T.ecb[:], 0.0, ["ecb"]),
+        lambda: vts(T.k64[:], T.kcol[:], 64.0, ALU.mult, None, None, ["kcol"], ["k64"]),
+        lambda: vms(T.Ct[:, 0:128:16], 0.5, ["Ct"]),
+        lambda: vms(T.ecb[:, 0:16:5], 1.0, ["ecb"]),
+        lambda: vcp(T.jc[:], T.iC[:], ["iC"], ["jc"]),
+        lambda: vts(T.base[:], T.iB[:], T.k64[:, 0:1], ALU.add, None, None, ["iB", "k64"], ["base"]),
+        lambda: vcp(T.ec[:], T.ecb[:], ["ecb"], ["ec"]),
+        lambda: vcp(T.onesh[:], T.ones[:], ["ones"], ["onesh"]),
+        lambda: vms(T.all16[:], -16.0, ["all16"]),
+    ]
+    vts(T.sgn[:], T.parI[:], 2.0, ALU.mult, -1.0, ALU.add, ["parI"], ["sgn"])
+    vcp(T.E[:], T.ledI[:], ["ledI"], ["E0", "E1"])
+    do(lists(), late[0:3])
+    signs()
+    neg("S", 1)
+    neg("V", 0)
+    do(late[3:10])
+    neg("V", 2)
+    do(late[10:])
+    neg("S", 3, 0, 320)
+    neg("V", 3, 320, 1024)
 
     def ce(i):
         return slice(i * 1024, (i + 1) * 1024)
@@ -302,11 +314,13 @@ def rank_program(g, core, T, topo):
 
     def scans(i):
         o = slice(i * 1024 + 16, (i + 1) * 1024 + 16)
-        op("V", lambda: V.tensor_tensor_scan(T.bb[:, o], T.Bb[:, ce(i)], T.zero[:], 0.0, ALU.add, ALU.max),
-           ["B%d" % i, "zero"], ["bb%d" % i])
         p = slice(i * 1024 + 15, (i + 1) * 1024 + 15)
-        op("V", lambda: V.tensor_tensor_scan(T.Qb[:, ce(i)], T.bb[:, p], T.Ab[:, ce(i)], 0.0, ALU.max, ALU.min),
-           ["bb%d" % i, "bbx" if i == 0 else "bb%d" % (i - 1), "A%d" % i], ["Q%d" % i])
+        return [
+            lambda: op("V", lambda: V.tensor_tensor_scan(T.bb[:, o], T.Bb[:, ce(i)], T.zero[:], 0.0, ALU.add, ALU.max),
+                       ["B%d" % i, "zero"], ["bb%d" % i]),
+            lambda: op("V", lambda: V.tensor_tensor_scan(T.Qb[:, ce(i)], T.bb[:, p], T.Ab[:, ce(i)], 0.0, ALU.max, ALU.min),
+                       ["bb%d" % i, "bbx" if i == 0 else "bb%d" % (i - 1), "A%d" % i], ["Q%d" % i]),
+        ]
 
     def over(q, i):
         if q == "V":
@@ -322,34 +336,43 @@ def rank_program(g, core, T, topo):
             return r
         op("P", f, R, W, B)
 
+    UB = (("pU0", 0), ("pU1", 0), ("pU0", 0), ("pU0", 64))
+
     def pU(i):
-        n = "pU%d" % (i % 2)
-        group([(T[n][:, 0:64], T.sel[:, 128 * k:128 * (k + 1)], T.Qb[:, i * 1024 + k:(i + 1) * 1024:16], k == 0, k == 15)
-               for k in range(16)], SEL + ["Q%d" % i], [n], [n])
+        n, o = UB[i]
+        group([(T[n][:, o:o + 64], T.sel[:, 128 * k:128 * (k + 1)], T.Qb[:, i * 1024 + k:(i + 1) * 1024:16], k == 0, k == 15)
+               for k in range(16)], SEL + ["Q%d" % i], ["u%d" % i], [n])
 
-    def hchain(i, t):
-        n = "pU%d" % (i % 2)
-        a = ca(i)
-        s = str(i)
-        e = "E%d" % (i // 2)
-        vts(T.uI[:, a], T[n][:, 0:64], T.sgn[:, 0:1], ALU.mult, None, None, [n, "sgn"], ["uI" + s], [n])
-        vts(T.uA[:, a], T.uI[:, a], 4095, ALU.bitwise_and, None, None, ["uI" + s], ["uA" + s])
-        vtt(T.eu[:, a], T.E[:, a], T.uA[:, a], ALU.mult, ["uA" + s, e], ["eu" + s])
-        vts(T.wv[:, a], T.eu[:, a], 5, ALU.arith_shift_right, 4095, ALU.bitwise_and, ["eu" + s], ["wv" + s])
+    def hchain(cs, t):
+        n = UB[cs[0]][0]
+        a = slice(cs[0] * 64, cs[-1] * 64 + 64)
+        p = T[n][:, 0:64 * len(cs)]
+        s = str(cs[0])
+        e = "E%d" % (cs[0] // 2)
         ek = T.E if t == 0 else T.Ek
-        vtt(T.hs[:, a], T.wv[:, a], ek[:, a], ALU.add, ["wv" + s, e if t == 0 else "Ek"], ["hs" + s])
-        vts(T.hI[:, a], T.hs[:, a], 4095, ALU.bitwise_and, None, None, ["hs" + s], ["hI" + s])
-        vts(T.LY[:, a], T.hI[:, a], T.offY[:, 0:1], ALU.add, None, None, ["hI" + s, "offY"], ["LY" + s])
+        return [
+            lambda: vts(T.uI[:, a], p, T.sgn[:, 0:1], ALU.mult, None, None, ["u%d" % i for i in cs] + ["sgn"], ["uI" + s], [n]),
+            lambda: vts(T.uA[:, a], T.uI[:, a], 4095, ALU.bitwise_and, None, None, ["uI" + s], ["uA" + s]),
+            lambda: vtt(T.eu[:, a], T.E[:, a], T.uA[:, a], ALU.mult, ["uA" + s, e], ["eu" + s]),
+            lambda: vts(T.wv[:, a], T.eu[:, a], 5, ALU.arith_shift_right, 4095, ALU.bitwise_and, ["eu" + s], ["wv" + s]),
+            lambda: vtt(T.hs[:, a], T.wv[:, a], ek[:, a], ALU.add, ["wv" + s, e if t == 0 else "Ek"], ["hs" + s]),
+            lambda: vts(T.hI[:, a], T.hs[:, a], 4095, ALU.bitwise_and, None, None, ["hs" + s], ["hI%d" % i for i in cs]),
+            lambda: vts(T.LY[:, a], T.hI[:, a], T.offY[:, 0:1], ALU.add, None, None, ["hI%d" % cs[0], "offY"],
+                        ["LY%d" % i for i in cs]),
+        ]
 
-    def ysub(i):
-        vtt(T.zb[:, ce(i)], T.XT[:, 0:GW].indirect(T.LY[:, ca(i)]), T.Qb[:, ce(i)], ALU.subtract,
-            ["LY%d" % i, "Q%d" % i] + XALL, ["z%d" % i])
+    def ysub(i, part=None):
+        lo, hi = (0, 64) if part is None else (32 * part, 32 * part + 32)
+        a = slice(i * 64 + lo, i * 64 + hi)
+        c = slice(a.start * 16, a.stop * 16)
+        vtt(T.zb[:, c], T.XT[:, 0:GW].indirect(T.LY[:, a]), T.Qb[:, c], ALU.subtract,
+            ["LY%d" % i, "Q%d" % i] + XALL, ["z%d" % i if part is None or part == 1 else "z%da" % i])
 
     def sign(q, i):
         if q == "V":
-            vts(T.sb[:, ce(i)], T.zb[:, ce(i)], -1.0, ALU.max, 1.0, ALU.min, ["z%d" % i], ["s%d" % i])
+            vts(T.sb[:, ce(i)], T.zb[:, ce(i)], -1.0, ALU.max, 1.0, ALU.min, ["z%d" % i, "z%da" % i], ["s%d" % i])
         else:
-            sact(T.sb[:, ce(i)], T.zb[:, ce(i)], ACT.Sign, ["z%d" % i], ["s%d" % i])
+            sact(T.sb[:, ce(i)], T.zb[:, ce(i)], ACT.Sign, ["z%d" % i, "z%da" % i], ["s%d" % i])
 
     def sums(ps, src, tag, b):
         group([(T[ps][:, b * 128 + k:(b + 1) * 128:16], src[:, b * 2048 + k:(b + 1) * 2048:16],
@@ -361,44 +384,56 @@ def rank_program(g, core, T, topo):
 
     def dec_over(b):
         s = str(b)
-        vts(T.ov[:, cb(b)], T.pOV[:, cb(b)], 8.5, ALU.is_ge, None, None, ["pOV" + s], ["ov" + s], ["pOV"])
-        vtt(T.gov[:, cb(b)], T.pGK[:, cb(b)], T.ov[:, cb(b)], ALU.mult, ["pGK", "ov" + s], ["gov" + s], ["pGK"])
+        return [
+            lambda: vts(T.ov[:, cb(b)], T.pOV[:, cb(b)], 8.5, ALU.is_ge, None, None, ["pOV" + s], ["ov" + s], ["pOV"]),
+            lambda: vtt(T.gov[:, cb(b)], T.pGK[:, cb(b)], T.ov[:, cb(b)], ALU.mult, ["pGK", "ov" + s], ["gov" + s], ["pGK"]),
+        ]
 
     def decide(b):
         s = str(b)
         c = cb(b)
-        vtt(T.comp[:, c], T.pS[:, c], T.gov[:, c], ALU.mult, ["pS" + s, "gov" + s], ["comp" + s], ["pS"])
-        op("V", lambda: V.tensor_tensor_scan(T.R1[:, c], T.Ct[:], T.comp[:, c], 0.5, ALU.min, ALU.max), ["Ct", "comp" + s],
-           ["R1" + s])
-        vcp(T.R1[:, b * 128:(b + 1) * 128:16], T.R1[:, b * 128 + 15:(b + 1) * 128:16], ["R1" + s], ["R1" + s])
-        op("V", lambda: V.tensor_tensor_scan(T.R2[:, c], T.Ct[:], T.R1[:, c], 0.5, ALU.min, ALU.max), ["Ct", "R1" + s],
-           ["R2" + s])
-        vtt(T.win[:, c], T.comp[:, c], T.R2[:, c], ALU.is_equal, ["comp" + s, "R2" + s], ["win" + s])
-        sact(T.flipX[:, c], T.R2[:, c], ACT.Sign, ["R2" + s, "half"], ["fl" + s], bias=T.Ct[:, 0:1] if False else -0.5)
-        group([(T.pWN[:, c], T.win[:, c], T.ident[:], True, True)], ["win" + s, "ident"], ["pWN" + s], ["pWN"])
-        calls = [(T.pZ[:, c], T.tri[:], T.flipX[:, c], True, False), (T.pZ[:, c], T.ones[:], T.crow[:], False, False)]
-        R = ["tri", "fl" + s, "ones", "crow"]
-        if b == 1:
-            calls.append((T.pZ[:, c], T.all16[:], T.flipX[:, cb(0)], False, False))
-            R += ["all16", "fl0"]
-        group(calls, R, ["pZ" + s], ["pZ"])
-        sact(T.wsb[:, c], T.pWN[:, c], ACT.Copy, ["pWN" + s], ["wsb" + s], ["pWN"])
-        group([(T.pZ[:, c], T.wsb[:, c], T.kmat[:], False, True)], ["wsb" + s, "kmat"], ["pZ" + s], ["pZ"])
+
+        def places():
+            sact(T.flipX[:, c], T.R2[:, c], ACT.Sign, ["R2" + s], ["fl" + s], bias=-0.5)
+
+        def winners():
+            vtt(T.win[:, c], T.comp[:, c], T.R2[:, c], ALU.is_equal, ["comp" + s, "R2" + s], ["win" + s])
+            group([(T.pWN[:, c], T.win[:, c], T.ident[:], True, True)], ["win" + s, "ident"], ["pWN" + s], ["pWN"])
+            calls = [(T.pZ[:, c], T.ones[:], T.crow[:], True, False), (T.pZ[:, c], T.tri[:], T.flipX[:, c], False, False)]
+            R = ["tri", "fl" + s, "ones", "crow"]
+            if b == 1:
+                calls.append((T.pZ[:, c], T.all16[:], T.flipX[:, cb(0)], False, False))
+                R += ["all16", "fl0"]
+            group(calls, R, ["pZ" + s], ["pZ"])
+            sact(T.wsb[:, c], T.pWN[:, c], ACT.Copy, ["pWN" + s], ["wsb" + s], ["pWN"])
+            group([(T.pZ[:, c], T.wsb[:, c], T.kmat[:], False, True)], ["wsb" + s, "kmat"], ["pZ" + s], ["pZ"])
+
+        def scan(dst, src, w, r):
+            op("V", lambda: V.tensor_tensor_scan(dst[:, c], T.Ct[:], src[:, c], 0.5, ALU.min, ALU.max), ["Ct", r], [w])
+
+        return [
+            lambda: vtt(T.comp[:, c], T.pS[:, c], T.gov[:, c], ALU.mult, ["pS" + s, "gov" + s], ["comp" + s], ["pS"]),
+            lambda: scan(T.R1, T.comp, "R1" + s, "comp" + s),
+            lambda: vcp(T.R1[:, b * 128:(b + 1) * 128:16], T.R1[:, b * 128 + 15:(b + 1) * 128:16], ["R1" + s], ["R1" + s]),
+            lambda: (scan(T.R2, T.R1, "R2" + s, "R1" + s), places()),
+            winners,
+        ]
 
     def clamps(b):
         s = str(b)
-        for c in range(4):
+
+        def one(c):
             lo = -(256.0 * c + 16)
             o = slice(c * 256 + b * 128, c * 256 + (b + 1) * 128)
             vts(T.D[:, o], T.pZ[:, cb(b)], lo, ALU.max, lo + 16, ALU.min, ["pZ" + s], ["D%d%d" % (c, b)], ["pZ"])
+        return [lambda c=c: one(c) for c in range(4)]
 
-    def pLJ():
-        calls = [(T.pSM[:, 0:4], T.onesh[:], T.jc[:], True, False)]
-        for b in range(2):
-            for c in range(4):
-                calls.append((T.pSM[:, 0:4], T.D[:, c * 256 + b * 128:c * 256 + (b + 1) * 128], T.ec[:, 4 * c:4 * c + 4], False,
-                              b == 1 and c == 3))
-        group(calls, ["onesh", "jc", "ec"] + ["D%d%d" % (c, b) for c in range(4) for b in range(2)], ["LJp"], ["pSM"])
+    def pLJ(b):
+        calls = [] if b else [(T.pSM[:, 0:4], T.onesh[:], T.jc[:], True, False)]
+        for c in range(4):
+            calls.append((T.pSM[:, 0:4], T.D[:, c * 256 + b * 128:c * 256 + (b + 1) * 128], T.ec[:, 4 * c:4 * c + 4], False,
+                          b == 1 and c == 3))
+        group(calls, ["onesh", "jc", "ec"] + ["D%d%d" % (c, b) for c in range(4)], ["LJp"], ["pSM"])
 
     def send(t):
         vcp(T.LJ[:], T.pSM[:, 0:4], ["LJp"], ["LJ"], ["pSM"])
@@ -411,37 +446,33 @@ def rank_program(g, core, T, topo):
         g.remote_dma(T["land%d" % t][:], T[qn][:], T.sem["arr%d" % t], T.sem.sent, pid, rid, sum(1 << e for e in eng))
         count["sent"] = count.get("sent", 0) + len(eng)
         src = T.cores[(rank - 1 - t % (n_ranks - 1)) % n_ranks]
-        note("R", "arr%d" % t, len(topo.engines(src, core)[:NENG]), [], ["land%d" % t], ())
-
-    known["R"] = {}
+        note("R", "arr%d" % t, len(topo.engines(src, core)[:NENG]), [], ["land%d" % t], (), {})
 
     def kappa():
-        group([(T.pSM[:, 16:24], T.ones[:], T.flipX[:, b * 128:(b + 1) * 128:16], b == 0, b == 1) for b in range(2)],
-              ["ones", "fl0", "fl1"], ["kp"], ["pSM"])
+        group([(T.pU1[:, 64:72], T.ones[:], T.flipX[:, b * 128:(b + 1) * 128:16], b == 0, b == 1) for b in range(2)],
+              ["ones", "fl0", "fl1"], ["kp"], ["pU1"])
 
     def kappa2():
-        op("V", lambda: V.tensor_reduce(T.kr[:], T.pSM[:, 16:24], AxisListType.X, ALU.add), ["kp"], ["kr"], ["pSM"])
-        vcp(T.kri[:], T.kr[:], ["kr"], ["kri"])
+        return [
+            lambda: op("V", lambda: V.tensor_reduce(T.kr[:], T.pU1[:, 64:72], AxisListType.X, ALU.add), ["kp"], ["kr"], ["pU1"]),
+            lambda: vcp(T.kri[:], T.kr[:], ["kr"], ["kri"]),
+            lambda: vts(T.krm[:], T.kri[:], 31, ALU.bitwise_and, None, None, ["kri"], ["krm"]),
+            lambda: vcp(T.kap[:], T.krm[:], ["krm"], ["kap"]),
+        ]
 
-    def update(last):
-        for b in range(2):
-            c = cb(b)
-            s = str(b)
-            vtt(T.dh[:, c], T.hI[:, c], T.E[:, c], ALU.subtract, ["hI%d" % (2 * b), "hI%d" % (2 * b + 1), "E" + s], ["dh" + s])
-            vtt(T.wM[:, c], T.pWN[:, c], T.sg[:, c], ALU.mult, ["pWN" + s, "sg" + s], ["wM" + s], ["pWN"])
-            vtt(T.wE[:, c], T.pWN[:, c], T.dh[:, c], ALU.mult, ["pWN" + s, "dh" + s], ["wE" + s], ["pWN"])
-            vtt(T.mB[:, c], T.mB[:, c], T.wM[:, c], ALU.add, ["mB" + s, "wM" + s], ["mB" + s])
-            vtt(T.E[:, c], T.E[:, c], T.wE[:, c], ALU.add, ["E" + s, "wE" + s], ["E" + s])
-        if last:
-            dma("Y", T.ym[:], T.mB[:], ["mB0", "mB1"], ["ym"])
-            dma("S", T.yl[:], T.E[:], ["E0", "E1"], ["yl"])
-            return
-        vts(T.krm[:], T.kri[:], 31, ALU.bitwise_and, None, None, ["kri"], ["krm"])
-        lists(full)
-        vts(T.sg[:], T.mB[:], -2.0, ALU.mult, 1.0, ALU.add, ["mB0", "mB1"], ["sg0", "sg1"])
-        vcp(T.kap[:], T.krm[:], ["krm"], ["kap"])
-        vts(T.Ek[:], T.E[:], T.kap[:, 0:1], ALU.add, None, None, ["E0", "E1", "kap"], ["Ek"])
-        pGK()
+    def ekappa():
+        sact(T.Ek[:], T.E[:], ACT.Identity, ["E0", "E1", "kap"], ["Ek"], bias=T.kap[:, 0:1])
+
+    def update(b):
+        c = cb(b)
+        s = str(b)
+        return [
+            lambda: vtt(T.dh[:, c], T.hI[:, c], T.E[:, c], ALU.subtract, ["hI%d" % (2 * b), "hI%d" % (2 * b + 1), "E" + s], ["dh" + s]),
+            lambda: vtt(T.wM[:, c], T.pWN[:, c], T.sg[:, c], ALU.mult, ["pWN" + s, "sg" + s], ["wM" + s], ["pWN"]),
+            lambda: vtt(T.wE[:, c], T.pWN[:, c], T.dh[:, c], ALU.mult, ["pWN" + s, "dh" + s], ["wE" + s], ["pWN"]),
+            lambda: vtt(T.mB[:, c], T.mB[:, c], T.wM[:, c], ALU.add, ["mB" + s, "wM" + s], ["mB" + s]),
+            lambda: vtt(T.E[:, c], T.E[:, c], T.wE[:, c], ALU.add, ["E" + s, "wE" + s], ["E" + s]),
+        ]
 
     def arrive(t, last):
         ln = "land%d" % t
@@ -453,77 +484,97 @@ def rank_program(g, core, T, topo):
         vtt(T.vbs[:], T.vinv[:], T.base[:], ALU.add, ["vinv", "base"], ["vbs"])
         vtt(T.vid[:], T.vm[:], T.vbs[:], ALU.add, ["vm", "vbs"], ["vid"])
         vcp(T.LI[:, 0:4], T.vid[:], ["vid"], ["LI"])
-        vts(T.LI[:, 4:8], T.vid[:], float(NOFF), ALU.add, None, None, ["vid"], ["LI2"])
+        if not last:
+            vts(T.LI[:, 4:8], T.vid[:], float(NOFF), ALU.add, None, None, ["vid"], ["LI2"])
         vtt(T.tx[:], T.XT[:, 0:TRO + 4096].indirect(T.LI[:, 0:4]), T[ln][:], ALU.add, ["LI", ln, "T1"] + XALL, ["tx"])
         vts(T.ND[:, 0:64], T.tx[:], 0.5, ALU.mult, -0.25, ALU.add, ["tx"], ["ND0"])
-        xw = XALL[:8] + ["T1"]
+        xw = XALL[:10] + ["T1"]
         if last:
             op("V", lambda: V.tensor_copy(T.XT[:, 0:WEND].indirect(T.LI[:, 0:4]), T.ND[:, 0:64]), ["LI", "ND0"], xw)
         else:
             vts(T.ND[:, 64:128], T.tx[:], -0.5, ALU.mult, 0.25, ALU.add, ["tx"], ["ND1"])
-            op("V", lambda: V.tensor_copy(T.XT[:, 0:WEND].indirect(T.LI[:, 0:8]), T.ND[:]), ["LI", "LI2", "ND0", "ND1"],
-               xw + ["C"])
+            op("V", lambda: V.tensor_copy(T.XT[:, 0:WEND].indirect(T.LI[:, 0:8]), T.ND[:]), ["LI", "LI2", "ND0", "ND1"], xw)
 
     for t in range(rounds):
         last = t == rounds - 1
         gA("V", 0)
         gB("S", 0)
-        gA("S", 1)
         gB("S", 1)
-        if t == 0:
-            late_constants()
-            pGK()
-        scans(0)
+        do(scans(0))
         pU(0)
-        over("V", 0)
+        gA("V", 1)
+        if t == 0:
+            pGK()
         gA("S", 2)
         gB("S", 2)
-        hchain(0, t)
-        ysub(0)
-        scans(1)
-        pU(1)
-        over("V", 1)
-        sums("pOV", T.pb, "p", 0)
-        sign("S", 0)
         gA("S", 3)
         gB("S", 3)
-        hchain(1, t)
-        scans(2)
+        h0 = hchain((0,), t)
+        do(h0[:3])
+        do(scans(1), h0[3:5])
+        pU(1)
+        do(h0[5:])
+        ysub(0)
+        over("S", 0)
+        over("S", 1)
+        sums("pOV", T.pb, "p", 0)
+        h1 = hchain((1,), t)
+        do(h1[:3])
+        do(scans(2), h1[3:5])
         pU(2)
+        do(h1[5:])
+        sign("S", 0)
+        do(scans(3))
+        pU(3)
         ysub(1)
         sign("S", 1)
         over("S", 2)
-        sums("pS", T.sb, "s", 0)
-        hchain(2, t)
-        scans(3)
-        pU(3)
-        ysub(2)
-        sign("S", 2)
         over("S", 3)
+        sums("pS", T.sb, "s", 0)
+        d0 = dec_over(0) + decide(0)
+        h23 = hchain((2, 3), t)
+        do(h23, d0[0:2])
+        ysub(2, 0)
+        d0[2]()
+        ysub(2, 1)
+        sign("S", 2)
+        d0[3]()
+        ysub(3, 0)
+        d0[4]()
         sums("pOV", T.pb, "p", 1)
-        dec_over(0)
-        decide(0)
-        hchain(3, t)
-        ysub(3)
+        d1 = dec_over(1) + decide(1)
+        d1[0]()
+        d0[5]()
+        d1[1]()
+        d0[6]()
+        ysub(3, 1)
+        u0 = update(0)
         sign("V", 3)
         sums("pS", T.sb, "s", 1)
-        clamps(0)
-        dec_over(1)
-        if t == 0:
-            trash_fill()
-        decide(1)
-        clamps(1)
-        pLJ()
+        do(clamps(0))
+        pLJ(0)
+        do(u0[0:1])
+        do(d1[2:], u0[1:])
+        do(clamps(1))
+        pLJ(1)
+        u1 = update(1)
         if not last:
             kappa()
+        do(u1[0:3])
         send(t)
-        if not last:
-            kappa2()
-        update(last)
+        do(u1[3:])
+        if last:
+            dma("Y", T.ym[:], T.mB[:], ["mB0", "mB1"], ["ym"])
+            dma("S", T.yl[:], T.E[:], ["E0", "E1"], ["yl"])
+        else:
+            do(lists(), kappa2())
+            signs()
+            ekappa()
+            pGK()
         arrive(t, last)
-    for b in range(4):
-        c = slice(b * 1024, (b + 1) * 1024)
-        dma("Y" if b % 2 == 0 else "S", T.yx[:, c], T.XT[:, c], ["X%d" % b], ["yx%d" % b])
+    for b in range(2):
+        c = slice(b * 2048, (b + 1) * 2048)
+        dma("YS"[b], T.yx[:, c], T.XT[:, c], ["X%d" % (2 * b), "X%d" % (2 * b + 1)], ["yx%d" % b])
     for sem, n in count.items():
         if known["G"].get(sem, 0) < n:
             g.wait_ge(T.sem[sem], n)

import numpy as np
from concourse.mybir import AluOpType as ALU, AxisListType, ActivationFunctionType as ACT

NX, NOFF, ZC, C15, TRO, WEND = 4096, 4096, 8192, 8193, 8208, 16400
GW = 8208
NENG = 8

SCRATCH = {
    "XT": ("sbuf", [128, WEND], "bfloat16"),
    "ledI": ("sbuf", [128, 256], "int32"),
    "E": ("sbuf", [128, 256], "float32"),
    "Ek": ("sbuf", [128, 256], "float32"),
    "mB": ("sbuf", [128, 256], "bfloat16"),
    "sg": ("sbuf", [128, 256], "bfloat16"),
    "LA": ("sbuf", [128, 256], "uint16"),
    "LB": ("sbuf", [128, 256], "uint16"),
    "LY": ("sbuf", [128, 256], "uint16"),
    "tE": ("sbuf", [128, 256], "float32"),
    "tM": ("sbuf", [128, 256], "float32"),
    "dh": ("sbuf", [128, 256], "float32"),
    "wE": ("sbuf", [128, 256], "float32"),
    "wM": ("sbuf", [128, 256], "bfloat16"),
    "Ab": ("sbuf", [128, 4096], "bfloat16"),
    "Bb": ("sbuf", [128, 4096], "bfloat16"),
    "bb": ("sbuf", [128, 4096 + 32], "bfloat16"),
    "Qb": ("sbuf", [128, 4096 + 16], "bfloat16"),
    "zb": ("sbuf", [128, 4096], "bfloat16"),
    "sb": ("sbuf", [128, 4096], "bfloat16"),
    "pb": ("sbuf", [128, 4096], "bfloat16"),
    "zero": ("sbuf", [128, 1024], "bfloat16"),
    "uI": ("sbuf", [128, 256], "int32"),
    "uA": ("sbuf", [128, 256], "int32"),
    "eu": ("sbuf", [128, 256], "int32"),
    "wv": ("sbuf", [128, 256], "int32"),
    "hs": ("sbuf", [128, 256], "int32"),
    "hI": ("sbuf", [128, 256], "int32"),
    "ov": ("sbuf", [128, 256], "bfloat16"),
    "gov": ("sbuf", [128, 256], "bfloat16"),
    "comp": ("sbuf", [128, 256], "float32"),
    "R1": ("sbuf", [128, 256], "float32"),
    "R2": ("sbuf", [128, 256], "float32"),
    "win": ("sbuf", [128, 256], "bfloat16"),
    "flipX": ("sbuf", [128, 256], "bfloat16"),
    "wsb": ("sbuf", [128, 256], "bfloat16"),
    "D": ("sbuf", [128, 1024], "float16"),
    "LJ": ("sbuf", [128, 4], "uint16"),
    "kr": ("sbuf", [128, 1], "float32"),
    "kri": ("sbuf", [128, 1], "int32"),
    "krm": ("sbuf", [128, 1], "int32"),
    "kap": ("sbuf", [128, 1], "float32"),
    "qs0": ("sbuf", [128, 64], "bfloat16"),
    "qs1": ("sbuf", [128, 64], "bfloat16"),
    "qs2": ("sbuf", [128, 64], "bfloat16"),
    "land0": ("sbuf", [128, 64], "bfloat16"),
    "land1": ("sbuf", [128, 64], "bfloat16"),
    "land2": ("sbuf", [128, 64], "bfloat16"),
    "vi": ("sbuf", [128, 4], "int32"),
    "vm": ("sbuf", [128, 4], "int32"),
    "vinv": ("sbuf", [128, 4], "float32"),
    "vbs": ("sbuf", [128, 4], "float32"),
    "vid": ("sbuf", [128, 4], "float32"),
    "LI": ("sbuf", [128, 8], "uint16"),
    "tx": ("sbuf", [128, 64], "float32"),
    "ND": ("sbuf", [128, 128], "int32"),
    "pI": ("sbuf", [128, 1], "int32"),
    "kI": ("sbuf", [128, 1], "int32"),
    "parI": ("sbuf", [128, 1], "int32"),
    "kcol": ("sbuf", [128, 1], "float32"),
    "sgn": ("sbuf", [128, 1], "float32"),
    "offY": ("sbuf", [128, 1], "float32"),
    "oB": ("sbuf", [128, 1], "float32"),
    "s2c": ("sbuf", [128, 1], "float32"),
    "s3c": ("sbuf", [128, 1], "float32"),
    "wcol": ("sbuf", [128, 1], "float32"),
    "w256": ("sbuf", [128, 1], "float32"),
    "k64": ("sbuf", [128, 1], "float32"),
    "i8": ("sbuf", [128, 8], "int32"),
    "i8s": ("sbuf", [128, 8], "int32"),
    "blkO": ("sbuf", [128, 8], "bfloat16"),
    "blkE": ("sbuf", [128, 8], "bfloat16"),
    "wb8": ("sbuf", [128, 8], "float32"),
    "iD": ("sbuf", [128, 128], "int32"),
    "iG": ("sbuf", [128, 128], "int32"),
    "iGs": ("sbuf", [128, 128], "int32"),
    "iR": ("sbuf", [128, 128], "int32"),
    "iB": ("sbuf", [128, 4], "int32"),
    "iC": ("sbuf", [128, 4], "int32"),
    "ident": ("sbuf", [128, 128], "bfloat16"),
    "tri": ("sbuf", [128, 128], "bfloat16"),
    "all16": ("sbuf", [128, 128], "bfloat16"),
    "ones": ("sbuf", [128, 128], "bfloat16"),
    "onesh": ("sbuf", [128, 128], "float16"),
    "kmat": ("sbuf", [128, 128], "bfloat16"),
    "Pd": ("sbuf", [128, 128], "bfloat16"),
    "crow": ("sbuf", [128, 128], "bfloat16"),
    "Ct": ("sbuf", [128, 128], "float32"),
    "base": ("sbuf", [128, 4], "float32"),
    "jc": ("sbuf", [128, 4], "float16"),
    "ecb": ("sbuf", [128, 16], "bfloat16"),
    "ec": ("sbuf", [128, 16], "float16"),
    "sel": ("sbuf", [128, 2048], "bfloat16"),
    "pU0": ("psum", [128, 512], "float32"),
    "pU1": ("psum", [128, 512], "float32"),
    "pOV": ("psum", [128, 512], "float32"),
    "pS": ("psum", [128, 512], "float32"),
    "pGK": ("psum", [128, 512], "float32"),
    "pWN": ("psum", [128, 512], "float32"),
    "pZ": ("psum", [128, 512], "float32"),
    "pSM": ("psum", [128, 512], "float32"),
}
SEMAPHORES = (["cV", "cS", "cP", "cG", "sent"] + ["arr%d" % t for t in range(3)] + ["d%d" % i for i in range(24)])


def rank_program(g, core, T, topo):
    rank = T.rank_of(core)
    if rank is None:
        return
    n_ranks = len(T.cores)
    rounds = 3
    V, S, P = g.vector, g.scalar, g.tensor
    Q = {"V": V, "S": S, "P": P, "G": g, "Y": g.sync}
    count = {}
    known = {q: {} for q in Q}
    lastw, readers, banks = {}, {}, {}
    seq, nd = [0], [0]

    def depends(q, R, W, B):
        toks = []
        for t in R:
            if t in lastw:
                toks.append(lastw[t])
        for t in W:
            if t in lastw:
                toks.append(lastw[t])
            toks += [x for x in readers.get(t, []) if x[2] != q]
        for b in B:
            toks += [x for qq, x in banks.get(b, {}).items() if qq != q]
        for sem, val, _, snap, _ in sorted(toks, key=lambda x: -x[4]):
            k = known[q]
            if k.get(sem, 0) >= val:
                continue
            Q[q].wait_ge(T.sem[sem], val)
            for s, v in snap.items():
                if k.get(s, 0) < v:
                    k[s] = v
            k[sem] = max(k.get(sem, 0), val)

    def note(q, sem, n, R, W, B, snap):
        count[sem] = count.get(sem, 0) + n
        seq[0] += 1
        tok = (sem, count[sem], q, snap, seq[0])
        for t in R:
            readers.setdefault(t, []).append(tok)
        for t in W:
            lastw[t] = tok
            readers[t] = []
        for b in B:
            banks.setdefault(b, {})[q] = tok

    def op(q, f, R, W, B=()):
        depends(q, R, W, B)
        f().then_inc(T.sem["c" + q], 1)
        note(q, "c" + q, 1, R, W, B, dict(known[q]))

    def dma(q, out, in_, R, W):
        depends(q, R, W, ())
        sem = "d%d" % nd[0]
        nd[0] += 1
        Q[q].dma_start(out, in_).then_inc(T.sem[sem], 16)
        note(q, sem, 16, R, W, (), dict(known[q]))

    def vts(out, in0, s1, o0, s2, o1, R, W, B=()):
        if o1 is None:
            op("V", lambda: V.tensor_scalar(out, in0, s1, None, o0), R, W, B)
        else:
            op("V", lambda: V.tensor_scalar(out, in0, s1, s2, o0, o1), R, W, B)

    def vtt(out, a, b, o, R, W, B=()):
        op("V", lambda: V.tensor_tensor(out, a, b, o), R, W, B)

    def vcp(out, in_, R, W, B=()):
        op("V", lambda: V.tensor_copy(out, in_), R, W, B)

    def vms(ap, c, W):
        op("V", lambda: V.memset(ap, c), [], W)

    def sact(out, in_, f, R, W, B=(), bias=0.0, scale=1.0):
        op("S", lambda: S.activation(out, in_, f, bias=bias, scale=scale), R, W, B)

    def iota(out, pat, base, cm, W, small=False):
        if small:
            op("G", lambda: g.iota(out, pat, base, cm, allow_small_or_imprecise_dtypes=True), [], W)
        else:
            op("G", lambda: g.iota(out, pat, base, cm), [], W)

    def do(*lists_):
        lists_ = [list(x) for x in lists_ if x]
        while lists_:
            for x in lists_:
                x.pop(0)()
            lists_ = [x for x in lists_ if x]

    dma("S", T.ledI[:], T.led[:], [], ["ledI"])
    for b in range(4):
        c = slice(b * 1024, (b + 1) * 1024)
        dma("Y", T.XT[:, c], T.xt[:, c], [], ["X%d" % b])
        if b == 0:
            dma("S", T.mB[:], T.mk[:], [], ["mB0", "mB1"])
    XALL = ["X0", "X1", "X2", "X3", "N0", "N1", "N2", "N3", "N1s", "N3s", "C"]

    iota(T.pI[:], [[0, 1]], 0, 1, ["pI"])
    iota(T.i8[:], [[-16, 8]], 0, 1, ["i8"])
    vms(T.ones[:], 1.0, ["ones"])
    vms(T.sel[:], 0.0, ["sel"])
    vts(T.kI[:], T.pI[:], 15, ALU.bitwise_and, None, None, ["pI"], ["kI"])
    vts(T.i8s[:], T.i8[:], 4, ALU.arith_shift_right, None, None, ["i8"], ["i8s"])
    vts(T.parI[:], T.kI[:], 1, ALU.bitwise_and, None, None, ["kI"], ["parI"])
    vcp(T.kcol[:], T.kI[:], ["kI"], ["kcol"])
    vts(T.blkO[:], T.i8s[:], 0, ALU.is_equal, None, None, ["i8s"], ["blkO"])
    vts(T.wcol[:], T.kI[:], 2.0, ALU.mult, 1.0, ALU.add, ["kI"], ["wcol"])
    vts(T.offY[:], T.parI[:], -float(NOFF), ALU.mult, float(NOFF), ALU.add, ["parI"], ["offY"])
    vts(T.oB[:], T.parI[:], float(NOFF), ALU.mult, -float(ZC), ALU.add, ["parI"], ["oB"])
    vts(T.wb8[:], T.blkO[:], T.wcol[:, 0:1], ALU.mult, None, None, ["blkO", "wcol"], ["wb8"])
    vts(T.s2c[:], T.kcol[:], 14.5, ALU.is_lt, None, None, ["kcol"], ["s2c"])
    vts(T.s3c[:], T.kcol[:], 14.5, ALU.is_ge, float(ZC), ALU.add, ["kcol"], ["s3c"])
    vms(T.XT[:, ZC:ZC + 16], 0.0, ["C"])
    vms(T.zero[:], 0.0, ["zero"])
    vms(T.XT[:, C15:C15 + 1], -2048.0, ["C"])
    vms(T.bb[:, 0:16], 0.0, ["bbx"])
    for b in range(8):
        sact(T.sel[:, 16 * b:16 * b + 129 * 15 + 1:129], T.ones[:, 0:16], ACT.Copy, ["ones", "wb8", "sel"], ["selg%d" % b],
             scale=T.wb8[:, b:b + 1])
    SEL = ["sel"] + ["selg%d" % b for b in range(8)]
    iota(T.iD[:], [[1, 128]], 0, -1, ["iD"])
    iota(T.iG[:], [[-16, 8], [0, 16]], 0, 1, ["iG"])
    iota(T.iR[:], [[0, 8], [1, 16]], 0, 0, ["iR"])
    iota(T.iB[:], [[1024, 4]], 0, 0, ["iB"])
    iota(T.iC[:], [[512, 4]], 32, 0, ["iC"])
    iota(T.Qb[:, 4096:4112], [[0, 16]], 256, 0, ["Qx"], True)
    iota(T.XT[:, TRO:TRO + 4096], [[0, 4096]], 0, 0, ["T1"], True)

    def lists(c=slice(0, 256)):
        return [
            lambda: vts(T.LA[:, c], T.E[:, c], T.offY[:, 0:1], ALU.add, None, None, ["E0", "E1", "offY"], ["LA"]),
            lambda: sact(T.tE[:, c], T.E[:, c], ACT.Identity, ["E0", "E1", "oB"], ["tE"], bias=T.oB[:, 0:1]),
            lambda: vtt(T.tM[:, c], T.tE[:, c], T.mB[:, c], ALU.mult, ["tE", "mB0", "mB1"], ["tM"]),
            lambda: vts(T.LB[:, c], T.tM[:, c], T.s2c[:, 0:1], ALU.mult, T.s3c[:, 0:1], ALU.add, ["tM", "s2c", "s3c"], ["LB"]),
        ]

    def signs():
        sact(T.sg[:], T.mB[:], ACT.Copy, ["mB0", "mB1"], ["sg0", "sg1"], bias=1.0, scale=-2.0)

    def neg(q, b, lo=0, hi=1024):
        c = slice(b * 1024 + lo, b * 1024 + hi)
        cn = slice(NOFF + b * 1024 + lo, NOFF + b * 1024 + hi)
        if q == "V":
            vts(T.XT[:, cn], T.XT[:, c], -1.0, ALU.mult, None, None, ["X%d" % b], ["N%d" % b])
        else:
            sact(T.XT[:, cn], T.XT[:, c], ACT.Copy, ["X%d" % b], ["N%ds" % b], scale=-1.0)

    late = [
        lambda: vts(T.w256[:], T.kcol[:], -1.0, ALU.mult, 256.0, ALU.add, ["kcol"], ["w256"]),
        lambda: vts(T.ident[:], T.iD[:], 0, ALU.is_equal, None, None, ["iD"], ["ident"]),
        lambda: vts(T.blkE[:], T.blkO[:], -1.0, ALU.mult, None, None, ["blkO"], ["blkE"]),
        lambda: vts(T.iGs[:], T.iG[:], 4, ALU.arith_shift_right, None, None, ["iG"], ["iGs"]),
        lambda: vts(T.Pd[:], T.ident[:], T.w256[:, 0:1], ALU.mult, None, None, ["ident", "w256"], ["Pd"]),
        lambda: vts(T.tri[:], T.iD[:], 0, ALU.is_ge, -16.0, ALU.mult, ["iD"], ["tri"]),
        lambda: vts(T.kmat[:], T.iGs[:], 0, ALU.is_equal, T.kcol[:, 0:1], ALU.mult, ["iGs", "kcol"], ["kmat"]),
        lambda: vts(T.crow[:], T.iR[:], 0.125, ALU.mult, None, None, ["iR"], ["crow"]),
        lambda: vms(T.Ct[:], 16384.0, ["Ct"]),
        lambda: vms(T.ecb[:], 0.0, ["ecb"]),
        lambda: vts(T.k64[:], T.kcol[:], 64.0, ALU.mult, None, None, ["kcol"], ["k64"]),
        lambda: vms(T.Ct[:, 0:128:16], 0.5, ["Ct"]),
        lambda: vms(T.ecb[:, 0:16:5], 1.0, ["ecb"]),
        lambda: vcp(T.jc[:], T.iC[:], ["iC"], ["jc"]),
        lambda: vts(T.base[:], T.iB[:], T.k64[:, 0:1], ALU.add, None, None, ["iB", "k64"], ["base"]),
        lambda: vcp(T.ec[:], T.ecb[:], ["ecb"], ["ec"]),
        lambda: vcp(T.onesh[:], T.ones[:], ["ones"], ["onesh"]),
        lambda: vms(T.all16[:], -16.0, ["all16"]),
    ]
    vts(T.sgn[:], T.parI[:], 2.0, ALU.mult, -1.0, ALU.add, ["parI"], ["sgn"])
    vcp(T.E[:], T.ledI[:], ["ledI"], ["E0", "E1"])
    do(lists(), late[0:3])
    signs()
    neg("S", 1)
    neg("V", 0)
    do(late[3:10])
    neg("V", 2)
    do(late[10:])
    neg("S", 3, 0, 320)
    neg("V", 3, 320, 1024)

    def ce(i):
        return slice(i * 1024, (i + 1) * 1024)

    def ca(i):
        return slice(i * 64, (i + 1) * 64)

    def cb(b):
        return slice(b * 128, (b + 1) * 128)

    def gather(q, out, lst, i, R, W):
        src = T.XT[:, 0:GW].indirect(lst[:, ca(i)])
        if q == "V":
            vcp(out[:, ce(i)], src, R + XALL, W)
        else:
            sact(out[:, ce(i)], src, ACT.Copy, R + XALL, W)

    def gA(q, i):
        gather(q, T.Ab, T.LA, i, ["LA"], ["A%d" % i])

    def gB(q, i):
        gather(q, T.Bb, T.LB, i, ["LB"], ["B%d" % i])

    def scans(i):
        o = slice(i * 1024 + 16, (i + 1) * 1024 + 16)
        p = slice(i * 1024 + 15, (i + 1) * 1024 + 15)
        return [
            lambda: op("V", lambda: V.tensor_tensor_scan(T.bb[:, o], T.Bb[:, ce(i)], T.zero[:], 0.0, ALU.add, ALU.max),
                       ["B%d" % i, "zero"], ["bb%d" % i]),
            lambda: op("V", lambda: V.tensor_tensor_scan(T.Qb[:, ce(i)], T.bb[:, p], T.Ab[:, ce(i)], 0.0, ALU.max, ALU.min),
                       ["bb%d" % i, "bbx" if i == 0 else "bb%d" % (i - 1), "A%d" % i], ["Q%d" % i]),
        ]

    def over(q, i):
        if q == "V":
            vts(T.pb[:, ce(i)], T.Qb[:, ce(i)], -1.0, ALU.max, 1.0, ALU.min, ["Q%d" % i], ["p%d" % i])
        else:
            sact(T.pb[:, ce(i)], T.Qb[:, ce(i)], ACT.Sign, ["Q%d" % i], ["p%d" % i])

    def group(calls, R, W, B):
        def f():
            r = None
            for c in calls:
                r = P.matmul(*c)
            return r
        op("P", f, R, W, B)

    UB = (("pU0", 0), ("pU1", 0), ("pU0", 0), ("pU0", 64))

    def pU(i):
        n, o = UB[i]
        group([(T[n][:, o:o + 64], T.sel[:, 128 * k:128 * (k + 1)], T.Qb[:, i * 1024 + k:(i + 1) * 1024:16], k == 0, k == 15)
               for k in range(16)], SEL + ["Q%d" % i], ["u%d" % i], [n])

    def hchain(cs, t):
        n = UB[cs[0]][0]
        a = slice(cs[0] * 64, cs[-1] * 64 + 64)
        p = T[n][:, 0:64 * len(cs)]
        s = str(cs[0])
        e = "E%d" % (cs[0] // 2)
        ek = T.E if t == 0 else T.Ek
        return [
            lambda: vts(T.uI[:, a], p, T.sgn[:, 0:1], ALU.mult, None, None, ["u%d" % i for i in cs] + ["sgn"], ["uI" + s], [n]),
            lambda: vts(T.uA[:, a], T.uI[:, a], 4095, ALU.bitwise_and, None, None, ["uI" + s], ["uA" + s]),
            lambda: vtt(T.eu[:, a], T.E[:, a], T.uA[:, a], ALU.mult, ["uA" + s, e], ["eu" + s]),
            lambda: vts(T.wv[:, a], T.eu[:, a], 5, ALU.arith_shift_right, 4095, ALU.bitwise_and, ["eu" + s], ["wv" + s]),
            lambda: vtt(T.hs[:, a], T.wv[:, a], ek[:, a], ALU.add, ["wv" + s, e if t == 0 else "Ek"], ["hs" + s]),
            lambda: vts(T.hI[:, a], T.hs[:, a], 4095, ALU.bitwise_and, None, None, ["hs" + s], ["hI%d" % i for i in cs]),
            lambda: vts(T.LY[:, a], T.hI[:, a], T.offY[:, 0:1], ALU.add, None, None, ["hI%d" % cs[0], "offY"],
                        ["LY%d" % i for i in cs]),
        ]

    def ysub(i, part=None):
        lo, hi = (0, 64) if part is None else (32 * part, 32 * part + 32)
        a = slice(i * 64 + lo, i * 64 + hi)
        c = slice(a.start * 16, a.stop * 16)
        vtt(T.zb[:, c], T.XT[:, 0:GW].indirect(T.LY[:, a]), T.Qb[:, c], ALU.subtract,
            ["LY%d" % i, "Q%d" % i] + XALL, ["z%d" % i if part is None or part == 1 else "z%da" % i])

    def sign(q, i):
        if q == "V":
            vts(T.sb[:, ce(i)], T.zb[:, ce(i)], -1.0, ALU.max, 1.0, ALU.min, ["z%d" % i, "z%da" % i], ["s%d" % i])
        else:
            sact(T.sb[:, ce(i)], T.zb[:, ce(i)], ACT.Sign, ["z%d" % i, "z%da" % i], ["s%d" % i])

    def sums(ps, src, tag, b):
        group([(T[ps][:, b * 128 + k:(b + 1) * 128:16], src[:, b * 2048 + k:(b + 1) * 2048:16],
                (T.blkE if k % 2 == 0 else T.blkO)[:], True, True) for k in range(16)],
              [tag + str(2 * b), tag + str(2 * b + 1), "blkE", "blkO"], [ps + str(b)], [ps])

    def pGK():
        group([(T.pGK[:, cb(b)], T.sg[:, cb(b)], T.Pd[:], True, True) for b in range(2)], ["sg0", "sg1", "Pd"], ["pGK"], ["pGK"])

    def dec_over(b):
        s = str(b)
        return [
            lambda: vts(T.ov[:, cb(b)], T.pOV[:, cb(b)], 8.5, ALU.is_ge, None, None, ["pOV" + s], ["ov" + s], ["pOV"]),
            lambda: vtt(T.gov[:, cb(b)], T.pGK[:, cb(b)], T.ov[:, cb(b)], ALU.mult, ["pGK", "ov" + s], ["gov" + s], ["pGK"]),
        ]

    def decide(b):
        s = str(b)
        c = cb(b)

        def places():
            sact(T.flipX[:, c], T.R2[:, c], ACT.Sign, ["R2" + s], ["fl" + s], bias=-0.5)

        def winners():
            vtt(T.win[:, c], T.comp[:, c], T.R2[:, c], ALU.is_equal, ["comp" + s, "R2" + s], ["win" + s])
            group([(T.pWN[:, c], T.win[:, c], T.ident[:], True, True)], ["win" + s, "ident"], ["pWN" + s], ["pWN"])
            calls = [(T.pZ[:, c], T.ones[:], T.crow[:], True, False), (T.pZ[:, c], T.tri[:], T.flipX[:, c], False, False)]
            R = ["tri", "fl" + s, "ones", "crow"]
            if b == 1:
                calls.append((T.pZ[:, c], T.all16[:], T.flipX[:, cb(0)], False, False))
                R += ["all16", "fl0"]
            group(calls, R, ["pZ" + s], ["pZ"])
            sact(T.wsb[:, c], T.pWN[:, c], ACT.Copy, ["pWN" + s], ["wsb" + s], ["pWN"])
            group([(T.pZ[:, c], T.wsb[:, c], T.kmat[:], False, True)], ["wsb" + s, "kmat"], ["pZ" + s], ["pZ"])

        def scan(dst, src, w, r):
            op("V", lambda: V.tensor_tensor_scan(dst[:, c], T.Ct[:], src[:, c], 0.5, ALU.min, ALU.max), ["Ct", r], [w])

        return [
            lambda: vtt(T.comp[:, c], T.pS[:, c], T.gov[:, c], ALU.mult, ["pS" + s, "gov" + s], ["comp" + s], ["pS"]),
            lambda: scan(T.R1, T.comp, "R1" + s, "comp" + s),
            lambda: vcp(T.R1[:, b * 128:(b + 1) * 128:16], T.R1[:, b * 128 + 15:(b + 1) * 128:16], ["R1" + s], ["R1" + s]),
            lambda: (scan(T.R2, T.R1, "R2" + s, "R1" + s), places()),
            winners,
        ]

    def clamps(b):
        s = str(b)

        def one(c):
            lo = -(256.0 * c + 16)
            o = slice(c * 256 + b * 128, c * 256 + (b + 1) * 128)
            vts(T.D[:, o], T.pZ[:, cb(b)], lo, ALU.max, lo + 16, ALU.min, ["pZ" + s], ["D%d%d" % (c, b)], ["pZ"])
        return [lambda c=c: one(c) for c in range(4)]

    def pLJ(b):
        calls = [] if b else [(T.pSM[:, 0:4], T.onesh[:], T.jc[:], True, False)]
        for c in range(4):
            calls.append((T.pSM[:, 0:4], T.D[:, c * 256 + b * 128:c * 256 + (b + 1) * 128], T.ec[:, 4 * c:4 * c + 4], False,
                          b == 1 and c == 3))
        group(calls, ["onesh", "jc", "ec"] + ["D%d%d" % (c, b) for c in range(4)], ["LJp"], ["pSM"])

    def send(t):
        vcp(T.LJ[:], T.pSM[:, 0:4], ["LJp"], ["LJ"], ["pSM"])
        qn = "qs%d" % t
        sact(T[qn][:], T.Qb[:].indirect(T.LJ[:, 0:4]), ACT.Abs, ["LJ", "Qx", "Q0", "Q1", "Q2", "Q3"], [qn])
        dst = T.cores[(rank + 1 + t % (n_ranks - 1)) % n_ranks]
        rid, pid, _ = topo.addr(dst)
        eng = topo.engines(core, dst)[:NENG]
        depends("G", [qn], [], ())
        g.remote_dma(T["land%d" % t][:], T[qn][:], T.sem["arr%d" % t], T.sem.sent, pid, rid, sum(1 << e for e in eng))
        count["sent"] = count.get("sent", 0) + len(eng)
        src = T.cores[(rank - 1 - t % (n_ranks - 1)) % n_ranks]
        note("R", "arr%d" % t, len(topo.engines(src, core)[:NENG]), [], ["land%d" % t], (), {})

    def kappa():
        group([(T.pU1[:, 64:72], T.ones[:], T.flipX[:, b * 128:(b + 1) * 128:16], b == 0, b == 1) for b in range(2)],
              ["ones", "fl0", "fl1"], ["kp"], ["pU1"])

    def kappa2():
        return [
            lambda: op("V", lambda: V.tensor_reduce(T.kr[:], T.pU1[:, 64:72], AxisListType.X, ALU.add), ["kp"], ["kr"], ["pU1"]),
            lambda: vcp(T.kri[:], T.kr[:], ["kr"], ["kri"]),
            lambda: vts(T.krm[:], T.kri[:], 31, ALU.bitwise_and, None, None, ["kri"], ["krm"]),
            lambda: vcp(T.kap[:], T.krm[:], ["krm"], ["kap"]),
        ]

    def ekappa():
        sact(T.Ek[:], T.E[:], ACT.Identity, ["E0", "E1", "kap"], ["Ek"], bias=T.kap[:, 0:1])

    def update(b):
        c = cb(b)
        s = str(b)
        return [
            lambda: vtt(T.dh[:, c], T.hI[:, c], T.E[:, c], ALU.subtract, ["hI%d" % (2 * b), "hI%d" % (2 * b + 1), "E" + s], ["dh" + s]),
            lambda: vtt(T.wM[:, c], T.pWN[:, c], T.sg[:, c], ALU.mult, ["pWN" + s, "sg" + s], ["wM" + s], ["pWN"]),
            lambda: vtt(T.wE[:, c], T.pWN[:, c], T.dh[:, c], ALU.mult, ["pWN" + s, "dh" + s], ["wE" + s], ["pWN"]),
            lambda: vtt(T.mB[:, c], T.mB[:, c], T.wM[:, c], ALU.add, ["mB" + s, "wM" + s], ["mB" + s]),
            lambda: vtt(T.E[:, c], T.E[:, c], T.wE[:, c], ALU.add, ["E" + s, "wE" + s], ["E" + s]),
        ]

    def arrive(t, last):
        ln = "land%d" % t
        group([(T.pSM[:, 32:36], T.sel[:, 128 * r:128 * (r + 1)], T[ln][:, r:64:16], r == 0, r == 15) for r in range(16)],
              SEL + [ln], ["pA"], ["pSM"])
        vcp(T.vi[:], T.pSM[:, 32:36], ["pA"], ["vi"], ["pSM"])
        vts(T.vinv[:], T.pSM[:, 32:36], 65535.5, ALU.is_ge, float(TRO), ALU.mult, ["pA"], ["vinv"], ["pSM"])
        vts(T.vm[:], T.vi[:], 63, ALU.bitwise_and, None, None, ["vi"], ["vm"])
        vtt(T.vbs[:], T.vinv[:], T.base[:], ALU.add, ["vinv", "base"], ["vbs"])
        vtt(T.vid[:], T.vm[:], T.vbs[:], ALU.add, ["vm", "vbs"], ["vid"])
        vcp(T.LI[:, 0:4], T.vid[:], ["vid"], ["LI"])
        if not last:
            vts(T.LI[:, 4:8], T.vid[:], float(NOFF), ALU.add, None, None, ["vid"], ["LI2"])
        vtt(T.tx[:], T.XT[:, 0:TRO + 4096].indirect(T.LI[:, 0:4]), T[ln][:], ALU.add, ["LI", ln, "T1"] + XALL, ["tx"])
        vts(T.ND[:, 0:64], T.tx[:], 0.5, ALU.mult, -0.25, ALU.add, ["tx"], ["ND0"])
        xw = XALL[:10] + ["T1"]
        if last:
            op("V", lambda: V.tensor_copy(T.XT[:, 0:WEND].indirect(T.LI[:, 0:4]), T.ND[:, 0:64]), ["LI", "ND0"], xw)
        else:
            vts(T.ND[:, 64:128], T.tx[:], -0.5, ALU.mult, 0.25, ALU.add, ["tx"], ["ND1"])
            op("V", lambda: V.tensor_copy(T.XT[:, 0:WEND].indirect(T.LI[:, 0:8]), T.ND[:]), ["LI", "LI2", "ND0", "ND1"], xw)

    for t in range(rounds):
        last = t == rounds - 1
        gA("V", 0)
        gB("S", 0)
        gB("S", 1)
        do(scans(0))
        pU(0)
        gA("V", 1)
        if t == 0:
            pGK()
        gA("S", 2)
        gB("S", 2)
        gA("S", 3)
        gB("S", 3)
        h0 = hchain((0,), t)
        do(h0[:3])
        do(scans(1), h0[3:5])
        pU(1)
        do(h0[5:])
        ysub(0)
        over("S", 0)
        over("S", 1)
        sums("pOV", T.pb, "p", 0)
        h1 = hchain((1,), t)
        do(h1[:3])
        do(scans(2), h1[3:5])
        pU(2)
        do(h1[5:])
        sign("S", 0)
        do(scans(3))
        pU(3)
        ysub(1)
        sign("S", 1)
        over("S", 2)
        over("S", 3)
        sums("pS", T.sb, "s", 0)
        d0 = dec_over(0) + decide(0)
        h23 = hchain((2, 3), t)
        do(h23, d0[0:2])
        ysub(2, 0)
        d0[2]()
        ysub(2, 1)
        sign("S", 2)
        d0[3]()
        ysub(3, 0)
        d0[4]()
        sums("pOV", T.pb, "p", 1)
        d1 = dec_over(1) + decide(1)
        d1[0]()
        d0[5]()
        d1[1]()
        d0[6]()
        ysub(3, 1)
        u0 = update(0)
        sign("V", 3)
        sums("pS", T.sb, "s", 1)
        do(clamps(0))
        pLJ(0)
        do(u0[0:1])
        do(d1[2:], u0[1:])
        do(clamps(1))
        pLJ(1)
        u1 = update(1)
        if not last:
            kappa()
        do(u1[0:3])
        send(t)
        do(u1[3:])
        if last:
            dma("Y", T.ym[:], T.mB[:], ["mB0", "mB1"], ["ym"])
            dma("S", T.yl[:], T.E[:], ["E0", "E1"], ["yl"])
        else:
            do(lists(), kappa2())
            signs()
            ekappa()
            pGK()
        arrive(t, last)
    for b in range(2):
        c = slice(b * 2048, (b + 1) * 2048)
        dma("YS"[b], T.yx[:, c], T.XT[:, c], ["X%d" % (2 * b), "X%d" % (2 * b + 1)], ["yx%d" % b])
    for sem, n in count.items():
        if known["G"].get(sem, 0) < n:
            g.wait_ge(T.sem[sem], n)
